import numpy as np
import ml_dtypes


def mxq(x, axis, fmt="e4m3"):
    dtype, down = {"e4m3": (ml_dtypes.float8_e4m3fn, 7), "e5m2": (ml_dtypes.float8_e5m2, 14)}[fmt]
    v = np.moveaxis(np.asarray(x, np.float32).astype(ml_dtypes.bfloat16).astype(np.float64), axis, -1)
    blocks = v.reshape(v.shape[:-1] + (-1, 32))
    amax = np.abs(blocks).max(-1, keepdims=True)
    byte = np.maximum(np.where(amax > 0, np.frexp(amax)[1] - 1 + 127, 0) - down, 1)
    scale = np.exp2(byte - 127.0)
    codes = (blocks / scale).astype(np.float32).astype(dtype).astype(np.float64)
    return np.moveaxis((codes * scale).reshape(v.shape), -1, axis)


WIDE = False


def mx_kscale(k):
    if not WIDE:
        return np.ones(k)
    levels = np.array([10, -10, 5, -5, 0])
    if k % 512:
        return np.exp2(np.random.permutation(np.resize(levels, k // 32))).repeat(32)
    a = np.empty((k // 512, 16))
    for p in range(k // 512):
        a[p, :8] = np.random.permutation(np.resize(levels, 8))
        for g in range(8):
            far = levels[np.abs(levels - a[p, g]) >= 10]
            a[p, g + 8] = far[np.random.randint(len(far))]
    return np.exp2(a.ravel()).repeat(32)


def f64(x):
    return np.asarray(x).astype(np.float64)


def striped(idx):
    return np.tile(idx.reshape(-1, 16).T, (8, 1)).astype(np.uint16)


def unstriped(offs):
    return offs[:16].T.reshape(-1).astype(np.int64)


E2M1 = np.array([0.0, 0.5, 1.0, 1.5, 2.0, 3.0, 4.0, 6.0, -0.0, -0.5, -1.0, -1.5, -2.0, -3.0, -4.0, -6.0])


def pack_weight(w, fmt):
    k, n = w.shape
    w = f64(np.asarray(w, np.float32).astype(ml_dtypes.bfloat16)).reshape(k // 32, 32, n)
    amax = np.abs(w).max(1)
    if fmt == "e4m3":
        byte = np.frexp(amax)[1] - 1 + 127 - 7
    else:
        mant, ex = np.frexp(amax / 6.0)
        byte = np.where(mant > 0.5, ex, ex - 1) + 127
    byte = np.clip(np.where(amax > 0, byte, 1), 1, 254)
    scaled = (w * np.exp2(127.0 - byte)[:, None, :]).reshape(k, n).astype(np.float32)
    by_word = np.ascontiguousarray(scaled.reshape(k // 512, 128, 4, n).transpose(0, 1, 3, 2))
    if fmt == "e4m3":
        words = by_word.astype(ml_dtypes.float8_e4m3fn).view(np.uint8)
    else:
        c = by_word.astype(ml_dtypes.float4_e2m1fn).view(np.uint8) & 0xF
        words = (c[..., 0::2] | (c[..., 1::2] << 4)).reshape(k // 512, 128, 2 * n)
    return np.ascontiguousarray(words), np.ascontiguousarray(byte.astype(np.uint8).reshape(k // 512, 16, n))


def unpack_weight(words, scales, fmt):
    g, _, n = scales.shape
    words = np.ascontiguousarray(words).reshape(g, 128, n, -1)
    if fmt == "e4m3":
        vals = words.view(ml_dtypes.float8_e4m3fn).astype(np.float64)
    else:
        nib = np.empty((g, 128, n, 4), np.uint8)
        nib[..., 0::2] = words & 0xF
        nib[..., 1::2] = words >> 4
        vals = E2M1[nib]
    vals = vals * np.repeat(np.exp2(scales.astype(np.float64) - 127.0), 8, axis=1)[..., None]
    return vals.transpose(0, 1, 3, 2).reshape(g * 512, n)


def gelu(v):
    return 0.5 * v * (1.0 + np.tanh(np.sqrt(2.0 / np.pi) * (v + 0.044715 * v**3)))


def bf(x):
    return np.asarray(x, np.float32).astype(ml_dtypes.bfloat16)

def planes(Y):
    n, m = Y.shape
    b = f64(bf(Y)).reshape(n // 32, 32, m)
    amax = np.abs(b).max(1)
    byte = np.clip(np.where(amax > 0, np.frexp(amax)[1] - 1 + 127 - 7, 1), 1, 254)
    codes = (b * np.exp2(127.0 - byte)[:, None, :]).reshape(n, m).astype(np.float32).astype(ml_dtypes.float8_e4m3fn).view(np.uint8)
    words = codes.reshape(n // 512, 128, 4, m).transpose(0, 1, 3, 2)
    return np.ascontiguousarray(words), np.ascontiguousarray(byte.astype(np.uint8).reshape(n // 512, 16, m))


K, T, S, T2, S2, N = 1024, 2048, 1024, 4096, 1024, 512

def setup_inputs():
    n = np.random.standard_normal
    s = mx_kscale(K)[:, None]
    u = mx_kscale(S)
    amp = np.exp(0.8 * n(N))
    tab_words, tab_scales = pack_weight(n((K, T)) * s / np.sqrt(K), "e4m3")
    tab2_words, tab2_scales = pack_weight(n((K, T2)) / s, "e4m3")
    w4_words, w4_scales = pack_weight(0.6 * n((K, N)) * s * amp / np.sqrt(K), "e2m1")
    w = n((S, N)) * amp / np.sqrt(S) / u[:, None]
    return {
        "tab_words": tab_words, "tab_scales": tab_scales,
        "tab2_words": tab2_words, "tab2_scales": tab2_scales,
        "offs": striped(np.random.permutation(T)[:S]),
        "offs2": striped(np.random.permutation(T2)[:S2]),
        "alpha": (np.exp(0.3 * n(S)) * u).astype(np.float32),
        "w": w.astype(np.float32),
        "w4_words": w4_words, "w4_scales": w4_scales,
        "b": (0.4 * n(N) * amp).astype(np.float32),
    }

def reference(tab_words, tab_scales, tab2_words, tab2_scales, offs, offs2, alpha, w, w4_words, w4_scales, b):
    v = unpack_weight(tab_words, tab_scales, "e4m3")[:, unstriped(offs)]
    v2 = unpack_weight(tab2_words, tab2_scales, "e4m3")[:, unstriped(offs2)]
    w4 = unpack_weight(w4_words, w4_scales, "e2m1")
    A = v.T @ v2
    e = np.log(1.0 + np.square(A)) * f64(alpha)[:, None]
    y = mxq(f64(w), 0, "e4m3").T @ mxq(e, 0, "e4m3") + w4.T @ v2
    y = y + f64(b)[:, None]
    words, scales = planes(y)
    return y, words, scales

@@ -1,0 +1,276 @@
+from contextlib import ExitStack
+
+import concourse.mybir as mybir
+from concourse.masks import make_identity
+
+K, T, S, T2, S2, N = 1024, 2048, 1024, 4096, 1024, 512
+FLOPS = 2 * K * S * S2 + 2 * S * N * S2 + 2 * K * N * S2
+
+F32 = mybir.dt.float32
+BF16 = mybir.dt.bfloat16
+I32 = mybir.dt.int32
+U32 = mybir.dt.uint32
+U16 = mybir.dt.uint16
+U8 = mybir.dt.uint8
+FP8X4 = mybir.dt.float8_e4m3fn_x4
+FP4X4 = mybir.dt.float4_e2m1fn_x4
+ACT = mybir.ActivationFunctionType
+MULT = mybir.AluOpType.mult
+ADD = mybir.AluOpType.add
+
+P = 128
+PACK = 4
+PASS = 512
+BANK = 512
+CHUNKS = (256, 256, 256, 128, 128)
+
+
+def tile_list_expert_patch_energies_kernel(
+    tc, tab_words, tab_scales, tab2_words, tab2_scales, offs, offs2, alpha, w, w4_words, w4_scales, b,
+    out_0, out_1, out_2,
+):
+    nc = tc.nc
+    with ExitStack() as ctx:
+        keep = ctx.enter_context(tc.tile_pool(name="keep", bufs=1))
+        late = ctx.enter_context(tc.tile_pool(name="late", bufs=1))
+        ring = ctx.enter_context(tc.tile_pool(name="ring", bufs=3))
+        psum = ctx.enter_context(tc.psum_pool(name="psum", bufs=4))
+
+        list1 = keep.tile([P, S // 16], U16, name="list1")
+        list2 = keep.tile([P, S2 // 16], U16, name="list2")
+        nc.sync.dma_start(list1[:], offs)
+        nc.sync.dma_start(list2[:], offs2)
+
+        win1 = keep.tile([P, T], U8, name="win1")
+        win2 = keep.tile([P, T2], U8, name="win2", tag="patch_pass1")
+        nc.vector.memset(win1[:].bitcast(I32), 0)
+        nc.vector.memset(win2[:].bitcast(I32), 0)
+        nc.scalar.dma_start(win1[0:P:4, :].bitcast(I32), tab_scales.rearrange("a q n -> q a n").bitcast(I32))
+        nc.scalar.dma_start(win2[0:P:4, :].bitcast(I32), tab2_scales.rearrange("a q n -> q a n").bitcast(I32))
+
+        ones = keep.tile([P, 1], F32, name="ones")
+        warm = keep.tile([P, 1], F32, name="warm")
+        nc.vector.memset(ones[:], 1.0)
+        nc.scalar.activation(warm[:], ones[:], ACT.Ln)
+
+        filt = keep.tile([P, 2 * T], I32, name="filt")
+        nc.sync.dma_start(
+            filt[:].rearrange("p (a n) -> p a n", a=2),
+            tab_words.rearrange("a p n i -> p a (n i)").bitcast(I32),
+        )
+        patch = [keep.tile([P, T2], I32, name="patch0")]
+        nc.sync.dma_start(patch[0][:], tab2_words[0].rearrange("p n i -> p (n i)").bitcast(I32))
+
+        v_sc = keep.tile([P, 2 * S], U8, name="v_sc", align_bytes=64)
+        v2_sc = keep.tile([P, 2 * S2], U8, name="v2_sc", align_bytes=64)
+        w4_sc_raw = keep.tile([P, 2 * N], U8, name="w4_sc_raw")
+        rows = keep.tile([P, P], F32, name="rows")
+        ident = keep.tile([P, P], F32, name="ident")
+        nc.vector.memset(rows[:], 0.0)
+        nc.vector.memset(v_sc[:].bitcast(I32), 0)
+        nc.vector.memset(v2_sc[:].bitcast(I32), 0)
+        nc.vector.memset(w4_sc_raw[:].bitcast(I32), 0)
+        make_identity(nc, ident[:])
+        for g in range(2):
+            nc.gpsimd.dma_start(
+                rows[PACK * g : PACK * (g + 1), :].rearrange("t (b r) -> t b r", r=8),
+                alpha[PASS * g : PASS * (g + 1)].rearrange("(b t r) -> t b r", t=PACK, r=8),
+            )
+        bias = keep.tile([P, PACK], F32, name="bias")
+        nc.gpsimd.dma_start(bias[:], b.rearrange("(p t) -> p t", t=PACK))
+        for q in range(4):
+            nc.gpsimd.dma_start(
+                w4_sc_raw[32 * q : 32 * q + 4, :].bitcast(I32).rearrange("r (a n) -> r a n", a=2),
+                w4_scales[:, 4 * q : 4 * q + 4, :].rearrange("a r n -> r a n").bitcast(I32),
+            )
+        turned = psum.tile([P, BANK], F32, name="turned", tag="a_bank")
+        nc.tensor.transpose(turned[:, 0:P], rows[:], ident[:])
+        alpha_col = keep.tile([P, 2 * PACK], F32, name="alpha_col")
+        nc.scalar.copy(alpha_col[:], turned[:, 0 : 2 * PACK])
+
+        def place(planes, picked):
+            for q in range(4):
+                nc.scalar.dma_start(
+                    planes[32 * q : 32 * q + 4, :].bitcast(I32).rearrange("r (a n) -> r a n", a=2),
+                    picked[32 * q : 32 * q + 32 : 4, :],
+                )
+
+        got1 = keep.tile([P, S], U8, name="got1")
+        nc.vector.tensor_copy(got1[:], win1[:].indirect(list1[:]))
+        dealt1 = keep.tile([P, S // 4], I32, name="dealt1")
+        nc.vector.tensor_copy(
+            dealt1[:].rearrange("p (g t b r) -> p g t b r", g=2, t=PACK, r=2),
+            got1[:].bitcast(I32).rearrange("p (g b t r) -> p g t b r", g=2, t=PACK, r=2),
+        )
+        place(v_sc, dealt1)
+        got2 = late.tile([P, 4 * 2 * PACK * N + 2 * 2 * N], U8, name="got2", offset=0)
+        nc.vector.tensor_copy(got2[:, 0:S2], win2[:].indirect(list2[:]))
+        place(v2_sc, got2[:, 0:S2].bitcast(I32))
+
+        patch.append(keep.tile([P, T2], I32, name="patch1", tag="patch_pass1"))
+        nc.sync.dma_start(patch[1][:], tab2_words[1].rearrange("p n i -> p (n i)").bitcast(I32))
+
+        v_w = {}
+        for g in range(2):
+            for a in range(2):
+                v_w[a, g] = keep.tile([P, PASS], U32, name="v_w%d%d" % (a, g), align_bytes=64)
+                nc.vector.tensor_copy(
+                    v_w[a, g][:].rearrange("p (t b r) -> p b t r", t=PACK, r=8),
+                    filt[:, a * T : (a + 1) * T].bitcast(U32).indirect(list1[:, 32 * g : 32 * (g + 1)]),
+                )
+        v2_w = {}
+        for a in range(2):
+            for h in range(2):
+                v2_w[a, h] = keep.tile([P, 512], U32, name="v2_w%d%d" % (a, h), align_bytes=64)
+                nc.vector.tensor_copy(
+                    v2_w[a, h][:], patch[a][:].bitcast(U32).indirect(list2[:, 32 * h : 32 * (h + 1)])
+                )
+
+        w4_raw = late.tile([P, 2 * N], U16, name="w4_raw", offset=4 * 2 * PACK * N)
+        nc.sync.dma_start(
+            w4_raw[:].bitcast(I32).rearrange("p (a n) -> p a n", a=2),
+            w4_words.rearrange("a p n -> p a n").bitcast(I32),
+        )
+        w_raw = []
+        for g in range(2):
+            w_raw.append(late.tile([P, PACK, N], F32, name="w_raw%d" % g, offset=4 * PACK * N * g))
+            dealt_rows = w[PASS * g : PASS * (g + 1), :].rearrange("(b t r) n -> t b r n", t=PACK, r=8)
+            for t in range(PACK):
+                nc.sync.dma_start(w_raw[g][:, t, :], dealt_rows[t])
+
+        w4_w = keep.tile([P, 2 * N], U16, name="w4_w", align_bytes=64)
+        w4_sc = keep.tile([P, 2 * N], U8, name="w4_sc", align_bytes=64)
+        w_w = keep.tile([P, 2 * N], U32, name="w_w", align_bytes=64)
+        w_sc = keep.tile([P, 2 * N], U8, name="w_sc", align_bytes=64)
+
+        def deal_w4():
+            nc.vector.tensor_copy(
+                w4_sc[:].rearrange("p (a t m) -> p a t m", a=2, t=PACK),
+                w4_sc_raw[:].rearrange("p (a m t) -> p a t m", a=2, t=PACK),
+            )
+            nc.vector.tensor_copy(
+                w4_w[:].rearrange("p (a t m) -> p a t m", a=2, t=PACK),
+                w4_raw[:].rearrange("p (a m t) -> p a t m", a=2, t=PACK),
+            )
+
+        def quantise_w():
+            w_bf = []
+            for g in range(2):
+                w_bf.append(keep.tile([P, PACK * N], BF16, name="w_bf%d" % g, align_bytes=64))
+                nc.vector.tensor_copy(
+                    w_bf[g][:].rearrange("p (t m s) -> p m t s", t=PACK, s=PACK),
+                    w_raw[g][:].rearrange("p s (m t) -> p m t s", t=PACK),
+                )
+            for g in range(2):
+                nc.vector.quantize_mx(
+                    w_w[:, N * g : N * (g + 1)].bitcast(FP8X4), w_sc[:, N * g : N * (g + 1)], w_bf[g][:]
+                )
+
+        def energies(j0, width):
+            h, jh = divmod(j0, 512)
+            made = []
+            for g in range(2):
+                sq = ring.tile([P, PACK * width], F32, name="sq", align_bytes=64)
+                for c in range(width // P):
+                    bank = psum.tile([P, BANK], F32, name="bank", tag="a_bank")
+                    for t in range(PACK):
+                        for a in range(2):
+                            i0 = S * a + PASS * g + P * t
+                            nc.tensor.matmul_mx(
+                                bank[:, P * t : P * (t + 1)],
+                                lhsT=v_w[a, g][:, P * t : P * (t + 1)].bitcast(FP8X4),
+                                lhsT_scale=v_sc[:, i0 : i0 + P],
+                                rhs=v2_w[a, h][:, jh + P * c : jh + P * (c + 1)].bitcast(FP8X4),
+                                rhs_scale=v2_sc[:, S2 * a + j0 + P * c : S2 * a + j0 + P * (c + 1)],
+                                start=(a == 0),
+                                stop=(a == 1),
+                            )
+                    nc.scalar.activation(
+                        sq[:, BANK * c : BANK * (c + 1)].rearrange("p (j t) -> p j t", t=PACK),
+                        bank[:].rearrange("p (t j) -> p j t", t=PACK),
+                        ACT.Square,
+                    )
+                ln = ring.tile([P, PACK * width], F32, name="ln", align_bytes=64)
+                nc.scalar.activation(ln[:], sq[:], ACT.Ln, bias=ones[:])
+                e_bf = ring.tile([P, PACK * width], BF16, name="e_bf", align_bytes=64)
+                nc.vector.tensor_tensor(
+                    e_bf[:].rearrange("p (j t) -> p j t", t=PACK),
+                    ln[:].rearrange("p (j t) -> p j t", t=PACK),
+                    alpha_col[:, PACK * g : PACK * (g + 1)].unsqueeze(1).to_broadcast([P, width, PACK]),
+                    MULT,
+                )
+                e_w = ring.tile([P, width], U32, name="e_w", align_bytes=64, bufs=4)
+                e_sc = ring.tile([P, width], U8, name="e_sc", align_bytes=64, bufs=4)
+                nc.vector.quantize_mx(e_w[:].bitcast(FP8X4), e_sc[:], e_bf[:])
+                made.append((e_w, e_sc))
+            return made
+
+        y_w = keep.tile([P, S2], U32, name="y_w", align_bytes=64)
+        y_sc = keep.tile([P, S2], U8, name="y_sc", align_bytes=64)
+        y_rows = out_0.rearrange("(p t) j -> p t j", t=PACK)
+        y_words = out_1[0].rearrange("p m t -> p (m t)").bitcast(I32)
+
+        def mix(j0, width, made):
+            h, jh = divmod(j0, 512)
+            per_bank = BANK // width
+            y = ring.tile([P, PACK, width], F32, name="y", align_bytes=64)
+            for t0 in range(0, PACK, per_bank):
+                bank = psum.tile([P, BANK], F32, name="y_bank", tag="y_bank")
+                first = True
+                for t in range(t0, t0 + per_bank):
+                    for a in range(2):
+                        n0 = N * a + P * t
+                        for c in range(width // P):
+                            col = width * (t - t0) + P * c
+                            nc.tensor.matmul_mx(
+                                bank[:, col : col + P],
+                                lhsT=w4_w[:, n0 : n0 + P].bitcast(U8).bitcast(FP4X4),
+                                lhsT_scale=w4_sc[:, n0 : n0 + P],
+                                rhs=v2_w[a, h][:, jh + P * c : jh + P * (c + 1)].bitcast(FP8X4),
+                                rhs_scale=v2_sc[:, S2 * a + j0 + P * c : S2 * a + j0 + P * (c + 1)],
+                                start=first,
+                                stop=False,
+                            )
+                            first = False
+                for g in range(2):
+                    for t in range(t0, t0 + per_bank):
+                        n0 = N * g + P * t
+                        nc.tensor.matmul_mx(
+                            bank[:, width * (t - t0) : width * (t - t0 + 1)],
+                            lhsT=w_w[:, n0 : n0 + P].bitcast(FP8X4),
+                            lhsT_scale=w_sc[:, n0 : n0 + P],
+                            rhs=made[g][0][:].bitcast(FP8X4),
+                            rhs_scale=made[g][1][:],
+                            start=False,
+                            stop=(g == 1 and t == t0 + per_bank - 1),
+                        )
+                for t in range(t0, t0 + per_bank):
+                    nc.scalar.activation(
+                        y[:, t, :], bank[:, width * (t - t0) : width * (t - t0 + 1)], ACT.Identity,
+                        bias=bias[:, t : t + 1],
+                    )
+            nc.sync.dma_start(y_rows[:, :, j0 : j0 + width], y[:])
+            y_bf = ring.tile([P, PACK * width], BF16, name="y_bf", align_bytes=64)
+            nc.vector.tensor_copy(
+                y_bf[:].rearrange("p (c i t) -> p c t i", t=PACK, i=4),
+                y[:].rearrange("p t (c i) -> p c t i", i=4),
+            )
+            nc.vector.quantize_mx(y_w[:, j0 : j0 + width].bitcast(FP8X4), y_sc[:, j0 : j0 + width], y_bf[:])
+            nc.sync.dma_start(y_words[:, j0 : j0 + width], y_w[:, j0 : j0 + width].bitcast(I32))
+
+        deal_w4()
+        starts = [sum(CHUNKS[:c]) for c in range(len(CHUNKS))]
+        before = None
+        for c, (j0, width) in enumerate(zip(starts, CHUNKS)):
+            made = energies(j0, width)
+            if c == 0:
+                quantise_w()
+            if before is not None:
+                mix(*before)
+            before = (j0, width, made)
+        mix(*before)
+        for q in range(4):
+            queue = nc.scalar if q % 2 else nc.sync
+            queue.dma_start(
+                out_2[0, 4 * q : 4 * q + 4, :].bitcast(I32), y_sc[32 * q : 32 * q + 4, :].bitcast(I32)
+            )

@@ -22,6 +22,11 @@ P = 128
 PACK = 4
 PASS = 512
 BANK = 512
+V_ALL = 0
+PATCH1 = V_ALL + 4 * 2 * S
+FILT1 = PATCH1 + 4 * T2
+PATCH0 = FILT1 + 4 * T
+LATE = PATCH0 + 4 * T2
 CHUNKS = (256, 256, 256, 128, 128)
 
 
@@ -42,23 +47,21 @@ def tile_list_expert_patch_energies_kernel(
         nc.sync.dma_start(list2[:], offs2)
 
         win1 = keep.tile([P, T], U8, name="win1")
-        win2 = keep.tile([P, T2], U8, name="win2", tag="patch_pass1")
+        win2 = late.tile([P, T2], U8, name="win2", offset=PATCH1 - T2 // 2)
         nc.vector.memset(win1[:].bitcast(I32), 0)
         nc.vector.memset(win2[:].bitcast(I32), 0)
         nc.scalar.dma_start(win1[0:P:4, :].bitcast(I32), tab_scales.rearrange("a q n -> q a n").bitcast(I32))
         nc.scalar.dma_start(win2[0:P:4, :].bitcast(I32), tab2_scales.rearrange("a q n -> q a n").bitcast(I32))
 
         ones = keep.tile([P, 1], F32, name="ones")
-        warm = keep.tile([P, 1], F32, name="warm")
+        warm = late.tile([P, 16], F32, name="warm", offset=PATCH0 - 32)
         nc.vector.memset(ones[:], 1.0)
-        nc.scalar.activation(warm[:], ones[:], ACT.Ln)
+        nc.scalar.activation(warm[:, 0:1], ones[:], ACT.Ln)
 
-        filt = keep.tile([P, 2 * T], I32, name="filt")
-        nc.sync.dma_start(
-            filt[:].rearrange("p (a n) -> p a n", a=2),
-            tab_words.rearrange("a p n i -> p a (n i)").bitcast(I32),
-        )
-        patch = [keep.tile([P, T2], I32, name="patch0")]
+        filt = [keep.tile([P, T], I32, name="filt0"), late.tile([P, T], I32, name="filt1", offset=FILT1)]
+        for a in range(2):
+            nc.sync.dma_start(filt[a][:], tab_words[a].rearrange("p n i -> p (n i)").bitcast(I32))
+        patch = [late.tile([P, T2], I32, name="patch0", offset=PATCH0)]
         nc.sync.dma_start(patch[0][:], tab2_words[0].rearrange("p n i -> p (n i)").bitcast(I32))
 
         v_sc = keep.tile([P, 2 * S], U8, name="v_sc", align_bytes=64)
@@ -88,9 +91,9 @@ def tile_list_expert_patch_energies_kernel(
         alpha_col = keep.tile([P, 2 * PACK], F32, name="alpha_col")
         nc.scalar.copy(alpha_col[:], turned[:, 0 : 2 * PACK])
 
-        def place(planes, picked):
+        def place(queue, planes, picked):
             for q in range(4):
-                nc.scalar.dma_start(
+                queue.dma_start(
                     planes[32 * q : 32 * q + 4, :].bitcast(I32).rearrange("r (a n) -> r a n", a=2),
                     picked[32 * q : 32 * q + 32 : 4, :],
                 )
@@ -102,38 +105,38 @@ def tile_list_expert_patch_energies_kernel(
             dealt1[:].rearrange("p (g t b r) -> p g t b r", g=2, t=PACK, r=2),
             got1[:].bitcast(I32).rearrange("p (g b t r) -> p g t b r", g=2, t=PACK, r=2),
         )
-        place(v_sc, dealt1)
-        got2 = late.tile([P, 4 * 2 * PACK * N + 2 * 2 * N], U8, name="got2", offset=0)
+        place(nc.scalar, v_sc, dealt1)
+        got2 = late.tile([P, 4 * 2 * PACK * N + 2 * 2 * N], U8, name="got2", offset=LATE)
         nc.vector.tensor_copy(got2[:, 0:S2], win2[:].indirect(list2[:]))
-        place(v2_sc, got2[:, 0:S2].bitcast(I32))
+        place(nc.scalar, v2_sc, got2[:, 0:S2].bitcast(I32))
 
-        patch.append(keep.tile([P, T2], I32, name="patch1", tag="patch_pass1"))
+
+        patch.append(late.tile([P, T2], I32, name="patch1", offset=PATCH1))
         nc.sync.dma_start(patch[1][:], tab2_words[1].rearrange("p n i -> p (n i)").bitcast(I32))
-
-        v_w = {}
+        v_all = late.tile([P, 2 * S], U32, name="v_all", offset=V_ALL, align_bytes=64)
+        v2_all = keep.tile([P, 2 * S2], U32, name="v2_all", align_bytes=64)
+        v_w = {(a, g): v_all[:, S * a + PASS * g : S * a + PASS * (g + 1)] for a in range(2) for g in range(2)}
+        v2_w = {(a, h): v2_all[:, S2 * a + 512 * h : S2 * a + 512 * (h + 1)] for a in range(2) for h in range(2)}
         for g in range(2):
             for a in range(2):
-                v_w[a, g] = keep.tile([P, PASS], U32, name="v_w%d%d" % (a, g), align_bytes=64)
                 nc.vector.tensor_copy(
-                    v_w[a, g][:].rearrange("p (t b r) -> p b t r", t=PACK, r=8),
-                    filt[:, a * T : (a + 1) * T].bitcast(U32).indirect(list1[:, 32 * g : 32 * (g + 1)]),
+                    v_w[a, g].rearrange("p (t b r) -> p b t r", t=PACK, r=8),
+                    filt[a][:].bitcast(U32).indirect(list1[:, 32 * g : 32 * (g + 1)]),
                 )
-        v2_w = {}
-        for a in range(2):
-            for h in range(2):
-                v2_w[a, h] = keep.tile([P, 512], U32, name="v2_w%d%d" % (a, h), align_bytes=64)
-                nc.vector.tensor_copy(
-                    v2_w[a, h][:], patch[a][:].bitcast(U32).indirect(list2[:, 32 * h : 32 * (h + 1)])
-                )
+        nc.vector.tensor_copy(v2_all[:, 0:S2], patch[0][:].bitcast(U32).indirect(list2[:]))
+        for h in range(2):
+            nc.vector.tensor_copy(
+                v2_w[1, h], patch[1][:].bitcast(U32).indirect(list2[:, 32 * h : 32 * (h + 1)])
+            )
 
-        w4_raw = late.tile([P, 2 * N], U16, name="w4_raw", offset=4 * 2 * PACK * N)
+        w4_raw = late.tile([P, 2 * N], U16, name="w4_raw", offset=LATE + 4 * 2 * PACK * N)
         nc.sync.dma_start(
             w4_raw[:].bitcast(I32).rearrange("p (a n) -> p a n", a=2),
             w4_words.rearrange("a p n -> p a n").bitcast(I32),
         )
         w_raw = []
         for g in range(2):
-            w_raw.append(late.tile([P, PACK, N], F32, name="w_raw%d" % g, offset=4 * PACK * N * g))
+            w_raw.append(late.tile([P, PACK, N], F32, name="w_raw%d" % g, offset=LATE + 4 * PACK * N * g))
             dealt_rows = w[PASS * g : PASS * (g + 1), :].rearrange("(b t r) n -> t b r n", t=PACK, r=8)
             for t in range(PACK):
                 nc.sync.dma_start(w_raw[g][:, t, :], dealt_rows[t])

@@ -23,11 +23,11 @@ PACK = 4
 PASS = 512
 BANK = 512
 V_ALL = 0
-PATCH1 = V_ALL + 4 * 2 * S
-FILT1 = PATCH1 + 4 * T2
-PATCH0 = FILT1 + 4 * T
-LATE = PATCH0 + 4 * T2
-CHUNKS = (256, 256, 256, 128, 128)
+PATCH0 = V_ALL + 4 * 2 * S
+PATCH1 = PATCH0 + 4 * T2
+LATE = PATCH1 + 4 * T2
+W4_RAW = LATE + 4 * 2 * PACK * N
+W4_SC_RAW = W4_RAW + 2 * 2 * N
 
 
 def tile_list_expert_patch_energies_kernel(
@@ -47,45 +47,42 @@ def tile_list_expert_patch_energies_kernel(
         nc.sync.dma_start(list2[:], offs2)
 
         win1 = keep.tile([P, T], U8, name="win1")
-        win2 = late.tile([P, T2], U8, name="win2", offset=PATCH1 - T2 // 2)
+        win2 = late.tile([P, T2], U8, name="win2", offset=V_ALL)
+        ones = keep.tile([P, 1], F32, name="ones")
+        nc.vector.memset(ones[:], 1.0)
+        rows = keep.tile([P, P], F32, name="rows")
         nc.vector.memset(win1[:].bitcast(I32), 0)
         nc.vector.memset(win2[:].bitcast(I32), 0)
-        nc.scalar.dma_start(win1[0:P:4, :].bitcast(I32), tab_scales.rearrange("a q n -> q a n").bitcast(I32))
-        nc.scalar.dma_start(win2[0:P:4, :].bitcast(I32), tab2_scales.rearrange("a q n -> q a n").bitcast(I32))
+        nc.vector.memset(rows[:], 0.0)
+        nc.sync.dma_start(win1[0:P:4, :].bitcast(I32), tab_scales.rearrange("a q n -> q a n").bitcast(I32))
+        nc.sync.dma_start(win2[0:P:4, :].bitcast(I32), tab2_scales.rearrange("a q n -> q a n").bitcast(I32))
 
-        ones = keep.tile([P, 1], F32, name="ones")
-        warm = late.tile([P, 16], F32, name="warm", offset=PATCH0 - 32)
-        nc.vector.memset(ones[:], 1.0)
+        warm = late.tile([P, 16], F32, name="warm", offset=PATCH1 - 32)
         nc.scalar.activation(warm[:, 0:1], ones[:], ACT.Ln)
 
-        filt = [keep.tile([P, T], I32, name="filt0"), late.tile([P, T], I32, name="filt1", offset=FILT1)]
-        for a in range(2):
-            nc.sync.dma_start(filt[a][:], tab_words[a].rearrange("p n i -> p (n i)").bitcast(I32))
-        patch = [late.tile([P, T2], I32, name="patch0", offset=PATCH0)]
-        nc.sync.dma_start(patch[0][:], tab2_words[0].rearrange("p n i -> p (n i)").bitcast(I32))
+        filt = keep.tile([P, 2 * T], I32, name="filt")
+        nc.sync.dma_start(
+            filt[:].rearrange("p (a n) -> p a n", a=2),
+            tab_words.rearrange("a p n i -> p a (n i)").bitcast(I32),
+        )
+        patch = []
+        for a, offset in enumerate((PATCH0, PATCH1)):
+            patch.append(late.tile([P, T2], I32, name="patch%d" % a, offset=offset))
+            nc.sync.dma_start(patch[a][:], tab2_words[a].rearrange("p n i -> p (n i)").bitcast(I32))
 
         v_sc = keep.tile([P, 2 * S], U8, name="v_sc", align_bytes=64)
         v2_sc = keep.tile([P, 2 * S2], U8, name="v2_sc", align_bytes=64)
-        w4_sc_raw = keep.tile([P, 2 * N], U8, name="w4_sc_raw")
-        rows = keep.tile([P, P], F32, name="rows")
         ident = keep.tile([P, P], F32, name="ident")
-        nc.vector.memset(rows[:], 0.0)
         nc.vector.memset(v_sc[:].bitcast(I32), 0)
         nc.vector.memset(v2_sc[:].bitcast(I32), 0)
-        nc.vector.memset(w4_sc_raw[:].bitcast(I32), 0)
         make_identity(nc, ident[:])
         for g in range(2):
-            nc.gpsimd.dma_start(
+            nc.scalar.dma_start(
                 rows[PACK * g : PACK * (g + 1), :].rearrange("t (b r) -> t b r", r=8),
                 alpha[PASS * g : PASS * (g + 1)].rearrange("(b t r) -> t b r", t=PACK, r=8),
             )
         bias = keep.tile([P, PACK], F32, name="bias")
         nc.gpsimd.dma_start(bias[:], b.rearrange("(p t) -> p t", t=PACK))
-        for q in range(4):
-            nc.gpsimd.dma_start(
-                w4_sc_raw[32 * q : 32 * q + 4, :].bitcast(I32).rearrange("r (a n) -> r a n", a=2),
-                w4_scales[:, 4 * q : 4 * q + 4, :].rearrange("a r n -> r a n").bitcast(I32),
-            )
         turned = psum.tile([P, BANK], F32, name="turned", tag="a_bank")
         nc.tensor.transpose(turned[:, 0:P], rows[:], ident[:])
         alpha_col = keep.tile([P, 2 * PACK], F32, name="alpha_col")
@@ -105,14 +102,12 @@ def tile_list_expert_patch_energies_kernel(
             dealt1[:].rearrange("p (g t b r) -> p g t b r", g=2, t=PACK, r=2),
             got1[:].bitcast(I32).rearrange("p (g b t r) -> p g t b r", g=2, t=PACK, r=2),
         )
-        place(nc.scalar, v_sc, dealt1)
-        got2 = late.tile([P, 4 * 2 * PACK * N + 2 * 2 * N], U8, name="got2", offset=LATE)
+        place(nc.gpsimd, v_sc, dealt1)
+        got2 = late.tile([P, W4_SC_RAW + 2 * N - LATE], U8, name="got2", offset=LATE)
         nc.vector.tensor_copy(got2[:, 0:S2], win2[:].indirect(list2[:]))
         place(nc.scalar, v2_sc, got2[:, 0:S2].bitcast(I32))
 
 
-        patch.append(late.tile([P, T2], I32, name="patch1", offset=PATCH1))
-        nc.sync.dma_start(patch[1][:], tab2_words[1].rearrange("p n i -> p (n i)").bitcast(I32))
         v_all = late.tile([P, 2 * S], U32, name="v_all", offset=V_ALL, align_bytes=64)
         v2_all = keep.tile([P, 2 * S2], U32, name="v2_all", align_bytes=64)
         v_w = {(a, g): v_all[:, S * a + PASS * g : S * a + PASS * (g + 1)] for a in range(2) for g in range(2)}
@@ -121,15 +116,22 @@ def tile_list_expert_patch_energies_kernel(
             for a in range(2):
                 nc.vector.tensor_copy(
                     v_w[a, g].rearrange("p (t b r) -> p b t r", t=PACK, r=8),
-                    filt[a][:].bitcast(U32).indirect(list1[:, 32 * g : 32 * (g + 1)]),
+                    filt[:, a * T : (a + 1) * T].bitcast(U32).indirect(list1[:, 32 * g : 32 * (g + 1)]),
                 )
-        nc.vector.tensor_copy(v2_all[:, 0:S2], patch[0][:].bitcast(U32).indirect(list2[:]))
-        for h in range(2):
-            nc.vector.tensor_copy(
-                v2_w[1, h], patch[1][:].bitcast(U32).indirect(list2[:, 32 * h : 32 * (h + 1)])
-            )
+        for a in range(2):
+            for h in range(2):
+                nc.vector.tensor_copy(
+                    v2_w[a, h], patch[a][:].bitcast(U32).indirect(list2[:, 32 * h : 32 * (h + 1)])
+                )
 
-        w4_raw = late.tile([P, 2 * N], U16, name="w4_raw", offset=LATE + 4 * 2 * PACK * N)
+        w4_sc_raw = late.tile([P, 2 * N], U8, name="w4_sc_raw", offset=W4_SC_RAW)
+        nc.gpsimd.memset(w4_sc_raw[:].bitcast(I32), 0)
+        for q in range(4):
+            nc.sync.dma_start(
+                w4_sc_raw[32 * q : 32 * q + 4, :].bitcast(I32).rearrange("r (a n) -> r a n", a=2),
+                w4_scales[:, 4 * q : 4 * q + 4, :].rearrange("a r n -> r a n").bitcast(I32),
+            )
+        w4_raw = late.tile([P, 2 * N], U16, name="w4_raw", offset=W4_RAW)
         nc.sync.dma_start(
             w4_raw[:].bitcast(I32).rearrange("p (a n) -> p a n", a=2),
             w4_words.rearrange("a p n -> p a n").bitcast(I32),
@@ -159,7 +161,9 @@ def tile_list_expert_patch_energies_kernel(
         def quantise_w():
             w_bf = []
             for g in range(2):
-                w_bf.append(keep.tile([P, PACK * N], BF16, name="w_bf%d" % g, align_bytes=64))
+                w_bf.append(late.tile(
+                    [P, PACK * N], BF16, name="w_bf%d" % g, align_bytes=64, offset=PATCH1 + 2 * PACK * N * g
+                ))
                 nc.vector.tensor_copy(
                     w_bf[g][:].rearrange("p (t m s) -> p m t s", t=PACK, s=PACK),
                     w_raw[g][:].rearrange("p s (m t) -> p m t s", t=PACK),
@@ -169,44 +173,52 @@ def tile_list_expert_patch_energies_kernel(
                     w_w[:, N * g : N * (g + 1)].bitcast(FP8X4), w_sc[:, N * g : N * (g + 1)], w_bf[g][:]
                 )
 
-        def energies(j0, width):
+        def responses(j0, width, groups):
             h, jh = divmod(j0, 512)
-            made = []
-            for g in range(2):
-                sq = ring.tile([P, PACK * width], F32, name="sq", align_bytes=64)
-                for c in range(width // P):
-                    bank = psum.tile([P, BANK], F32, name="bank", tag="a_bank")
+            units = [(g, c0) for g in groups for c0 in range(0, width, P)]
+            banks = [psum.tile([P, BANK], F32, name="bank", tag="a_bank") for unit in units]
+            for a in range(2):
+                for (g, c0), bank in zip(units, banks):
                     for t in range(PACK):
-                        for a in range(2):
-                            i0 = S * a + PASS * g + P * t
-                            nc.tensor.matmul_mx(
-                                bank[:, P * t : P * (t + 1)],
-                                lhsT=v_w[a, g][:, P * t : P * (t + 1)].bitcast(FP8X4),
-                                lhsT_scale=v_sc[:, i0 : i0 + P],
-                                rhs=v2_w[a, h][:, jh + P * c : jh + P * (c + 1)].bitcast(FP8X4),
-                                rhs_scale=v2_sc[:, S2 * a + j0 + P * c : S2 * a + j0 + P * (c + 1)],
-                                start=(a == 0),
-                                stop=(a == 1),
-                            )
-                    nc.scalar.activation(
-                        sq[:, BANK * c : BANK * (c + 1)].rearrange("p (j t) -> p j t", t=PACK),
-                        bank[:].rearrange("p (t j) -> p j t", t=PACK),
-                        ACT.Square,
-                    )
-                ln = ring.tile([P, PACK * width], F32, name="ln", align_bytes=64)
-                nc.scalar.activation(ln[:], sq[:], ACT.Ln, bias=ones[:])
-                e_bf = ring.tile([P, PACK * width], BF16, name="e_bf", align_bytes=64)
-                nc.vector.tensor_tensor(
-                    e_bf[:].rearrange("p (j t) -> p j t", t=PACK),
-                    ln[:].rearrange("p (j t) -> p j t", t=PACK),
-                    alpha_col[:, PACK * g : PACK * (g + 1)].unsqueeze(1).to_broadcast([P, width, PACK]),
-                    MULT,
+                        i0 = S * a + PASS * g + P * t
+                        nc.tensor.matmul_mx(
+                            bank[:, P * t : P * (t + 1)],
+                            lhsT=v_w[a, g][:, P * t : P * (t + 1)].bitcast(FP8X4),
+                            lhsT_scale=v_sc[:, i0 : i0 + P],
+                            rhs=v2_w[a, h][:, jh + c0 : jh + c0 + P].bitcast(FP8X4),
+                            rhs_scale=v2_sc[:, S2 * a + j0 + c0 : S2 * a + j0 + c0 + P],
+                            start=(a == 0 and t == 0),
+                            stop=(a == 1 and t == PACK - 1),
+                        )
+            return banks
+
+        def energies(j0, width, groups, banks=None):
+            cols = PACK * width * len(groups)
+            sq = ring.tile([P, cols], F32, name="sq", align_bytes=64, bufs=2)
+            for u, (g, c0) in enumerate([(g, c0) for g in groups for c0 in range(0, width, P)]):
+                bank = banks[u] if banks else responses(j0 + c0, P, (g,))[0]
+                nc.scalar.activation(
+                    sq[:, BANK * u : BANK * (u + 1)].rearrange("p (j t) -> p j t", t=PACK),
+                    bank[:].rearrange("p (t j) -> p j t", t=PACK),
+                    ACT.Square,
                 )
-                e_w = ring.tile([P, width], U32, name="e_w", align_bytes=64, bufs=4)
-                e_sc = ring.tile([P, width], U8, name="e_sc", align_bytes=64, bufs=4)
-                nc.vector.quantize_mx(e_w[:].bitcast(FP8X4), e_sc[:], e_bf[:])
-                made.append((e_w, e_sc))
-            return made
+            ln = ring.tile([P, cols], F32, name="ln", align_bytes=64)
+            nc.scalar.activation(ln[:], sq[:], ACT.Ln, bias=ones[:])
+            e_bf = ring.tile([P, cols], BF16, name="e_bf", align_bytes=64, bufs=2)
+            gains = alpha_col[:, PACK * groups[0] : PACK * (groups[-1] + 1)].rearrange("p (g t) -> p g t", t=PACK)
+            nc.vector.tensor_tensor(
+                e_bf[:].rearrange("p (g j t) -> p g j t", g=len(groups), t=PACK),
+                ln[:].rearrange("p (g j t) -> p g j t", g=len(groups), t=PACK),
+                gains.unsqueeze(2).to_broadcast([P, len(groups), width, PACK]),
+                MULT,
+            )
+            e_w = ring.tile([P, cols // PACK], U32, name="e_w", align_bytes=64, bufs=5)
+            e_sc = ring.tile([P, cols // PACK], U8, name="e_sc", align_bytes=64, bufs=5)
+            nc.vector.quantize_mx(e_w[:].bitcast(FP8X4), e_sc[:], e_bf[:])
+            return [
+                (j0, width, g, e_w[:, width * u : width * (u + 1)], e_sc[:, width * u : width * (u + 1)])
+                for u, g in enumerate(groups)
+            ]
 
         y_w = keep.tile([P, S2], U32, name="y_w", align_bytes=64)
         y_sc = keep.tile([P, S2], U8, name="y_sc", align_bytes=64)
@@ -216,37 +228,38 @@ def tile_list_expert_patch_energies_kernel(
         def mix(j0, width, made):
             h, jh = divmod(j0, 512)
             per_bank = BANK // width
+            step = BANK if width == BANK else P
             y = ring.tile([P, PACK, width], F32, name="y", align_bytes=64)
             for t0 in range(0, PACK, per_bank):
                 bank = psum.tile([P, BANK], F32, name="y_bank", tag="y_bank")
-                first = True
+                passes = []
                 for t in range(t0, t0 + per_bank):
                     for a in range(2):
                         n0 = N * a + P * t
-                        for c in range(width // P):
-                            col = width * (t - t0) + P * c
-                            nc.tensor.matmul_mx(
-                                bank[:, col : col + P],
-                                lhsT=w4_w[:, n0 : n0 + P].bitcast(U8).bitcast(FP4X4),
-                                lhsT_scale=w4_sc[:, n0 : n0 + P],
-                                rhs=v2_w[a, h][:, jh + P * c : jh + P * (c + 1)].bitcast(FP8X4),
-                                rhs_scale=v2_sc[:, S2 * a + j0 + P * c : S2 * a + j0 + P * (c + 1)],
-                                start=first,
-                                stop=False,
-                            )
-                            first = False
-                for g in range(2):
+                        for c0 in range(0, width, step):
+                            passes.append((
+                                bank[:, width * (t - t0) + c0 : width * (t - t0) + c0 + step],
+                                w4_w[:, n0 : n0 + P].bitcast(U8).bitcast(FP4X4),
+                                w4_sc[:, n0 : n0 + P],
+                                v2_w[a, h][:, jh + c0 : jh + c0 + step].bitcast(FP8X4),
+                                v2_sc[:, S2 * a + j0 + c0 : S2 * a + j0 + c0 + step],
+                            ))
+                for je, we, g, e_w, e_sc in made:
                     for t in range(t0, t0 + per_bank):
                         n0 = N * g + P * t
-                        nc.tensor.matmul_mx(
-                            bank[:, width * (t - t0) : width * (t - t0 + 1)],
-                            lhsT=w_w[:, n0 : n0 + P].bitcast(FP8X4),
-                            lhsT_scale=w_sc[:, n0 : n0 + P],
-                            rhs=made[g][0][:].bitcast(FP8X4),
-                            rhs_scale=made[g][1][:],
-                            start=False,
-                            stop=(g == 1 and t == t0 + per_bank - 1),
-                        )
+                        col = width * (t - t0) + je - j0
+                        passes.append((
+                            bank[:, col : col + we],
+                            w_w[:, n0 : n0 + P].bitcast(FP8X4),
+                            w_sc[:, n0 : n0 + P],
+                            e_w.bitcast(FP8X4),
+                            e_sc,
+                        ))
+                for n, (dst, lhs, lhs_sc, rhs, rhs_sc) in enumerate(passes):
+                    nc.tensor.matmul_mx(
+                        dst, lhsT=lhs, lhsT_scale=lhs_sc, rhs=rhs, rhs_scale=rhs_sc,
+                        start=(n == 0), stop=(n == len(passes) - 1),
+                    )
                 for t in range(t0, t0 + per_bank):
                     nc.scalar.activation(
                         y[:, t, :], bank[:, width * (t - t0) : width * (t - t0 + 1)], ACT.Identity,
@@ -262,16 +275,17 @@ def tile_list_expert_patch_energies_kernel(
             nc.sync.dma_start(y_words[:, j0 : j0 + width], y_w[:, j0 : j0 + width].bitcast(I32))
 
         deal_w4()
-        starts = [sum(CHUNKS[:c]) for c in range(len(CHUNKS))]
-        before = None
-        for c, (j0, width) in enumerate(zip(starts, CHUNKS)):
-            made = energies(j0, width)
-            if c == 0:
-                quantise_w()
-            if before is not None:
-                mix(*before)
-            before = (j0, width, made)
-        mix(*before)
+        banks = responses(0, 256, (0, 1))
+        made = energies(0, 256, (0,), banks[:2]) + energies(0, 256, (1,), banks[2:])
+        quantise_w()
+        made = made + energies(256, 256, (0, 1))
+        third = energies(512, 256, (0, 1))
+        mix(0, 512, made)
+        made = energies(768, 128, (0, 1))
+        mix(512, 256, third)
+        last = energies(896, 128, (0,)) + energies(896, 128, (1,))
+        mix(768, 128, made)
+        mix(896, 128, last)
         for q in range(4):
             queue = nc.scalar if q % 2 else nc.sync
             queue.dma_start(

@@ -22,9 +22,9 @@ P = 128
 PACK = 4
 PASS = 512
 BANK = 512
+ROW0 = 96
 V_ALL = 0
-PATCH0 = V_ALL + 4 * 2 * S
-PATCH1 = PATCH0 + 4 * T2
+PATCH1 = V_ALL + 4 * 2 * S
 LATE = PATCH1 + 4 * T2
 W4_RAW = LATE + 4 * 2 * PACK * N
 W4_SC_RAW = W4_RAW + 2 * 2 * N
@@ -43,37 +43,32 @@ def tile_list_expert_patch_energies_kernel(
 
         list1 = keep.tile([P, S // 16], U16, name="list1")
         list2 = keep.tile([P, S2 // 16], U16, name="list2")
-        nc.sync.dma_start(list1[:], offs)
-        nc.sync.dma_start(list2[:], offs2)
-
         win1 = keep.tile([P, T], U8, name="win1")
         win2 = late.tile([P, T2], U8, name="win2", offset=V_ALL)
+        nc.sync.dma_start(list1[:], offs)
+        nc.sync.dma_start(win1[ROW0:P, :].bitcast(I32), tab_scales.rearrange("a q n -> q a n").bitcast(I32))
+        nc.sync.dma_start(list2[:], offs2)
+        nc.sync.dma_start(win2[ROW0:P, :].bitcast(I32), tab2_scales.rearrange("a q n -> q a n").bitcast(I32))
         ones = keep.tile([P, 1], F32, name="ones")
         nc.vector.memset(ones[:], 1.0)
         rows = keep.tile([P, P], F32, name="rows")
-        nc.vector.memset(win1[:].bitcast(I32), 0)
-        nc.vector.memset(win2[:].bitcast(I32), 0)
         nc.vector.memset(rows[:], 0.0)
-        nc.sync.dma_start(win1[0:P:4, :].bitcast(I32), tab_scales.rearrange("a q n -> q a n").bitcast(I32))
-        nc.sync.dma_start(win2[0:P:4, :].bitcast(I32), tab2_scales.rearrange("a q n -> q a n").bitcast(I32))
-
-        warm = late.tile([P, 16], F32, name="warm", offset=PATCH1 - 32)
-        nc.scalar.activation(warm[:, 0:1], ones[:], ACT.Ln)
+        nc.vector.memset(win1[0:ROW0, :].bitcast(I32), 0)
+        nc.vector.memset(win2[0:ROW0, :].bitcast(I32), 0)
+        zero = keep.tile([P, 1], F32, name="zero")
+        nc.scalar.activation(zero[:], ones[:], ACT.Ln)
 
         filt = keep.tile([P, 2 * T], I32, name="filt")
         nc.sync.dma_start(
             filt[:].rearrange("p (a n) -> p a n", a=2),
             tab_words.rearrange("a p n i -> p a (n i)").bitcast(I32),
         )
-        patch = []
-        for a, offset in enumerate((PATCH0, PATCH1)):
-            patch.append(late.tile([P, T2], I32, name="patch%d" % a, offset=offset))
+        patch = [keep.tile([P, T2], I32, name="patch0"), late.tile([P, T2], I32, name="patch1", offset=PATCH1)]
+        for a in range(2):
             nc.sync.dma_start(patch[a][:], tab2_words[a].rearrange("p n i -> p (n i)").bitcast(I32))
 
-        v_sc = keep.tile([P, 2 * S], U8, name="v_sc", align_bytes=64)
         v2_sc = keep.tile([P, 2 * S2], U8, name="v2_sc", align_bytes=64)
         ident = keep.tile([P, P], F32, name="ident")
-        nc.vector.memset(v_sc[:].bitcast(I32), 0)
         nc.vector.memset(v2_sc[:].bitcast(I32), 0)
         make_identity(nc, ident[:])
         for g in range(2):
@@ -88,11 +83,11 @@ def tile_list_expert_patch_energies_kernel(
         alpha_col = keep.tile([P, 2 * PACK], F32, name="alpha_col")
         nc.scalar.copy(alpha_col[:], turned[:, 0 : 2 * PACK])
 
-        def place(queue, planes, picked):
-            for q in range(4):
+        def place(queue, row, picked):
+            for q in (0, 2, 1, 3):
                 queue.dma_start(
-                    planes[32 * q : 32 * q + 4, :].bitcast(I32).rearrange("r (a n) -> r a n", a=2),
-                    picked[32 * q : 32 * q + 32 : 4, :],
+                    v2_sc[32 * q + row : 32 * q + row + 4, :].bitcast(I32).rearrange("r (a n) -> r a n", a=2),
+                    picked[ROW0 + 8 * q : ROW0 + 8 * (q + 1), :],
                 )
 
         got1 = keep.tile([P, S], U8, name="got1")
@@ -102,10 +97,10 @@ def tile_list_expert_patch_energies_kernel(
             dealt1[:].rearrange("p (g t b r) -> p g t b r", g=2, t=PACK, r=2),
             got1[:].bitcast(I32).rearrange("p (g b t r) -> p g t b r", g=2, t=PACK, r=2),
         )
-        place(nc.gpsimd, v_sc, dealt1)
+        place(nc.gpsimd, 4, dealt1)
         got2 = late.tile([P, W4_SC_RAW + 2 * N - LATE], U8, name="got2", offset=LATE)
         nc.vector.tensor_copy(got2[:, 0:S2], win2[:].indirect(list2[:]))
-        place(nc.scalar, v2_sc, got2[:, 0:S2].bitcast(I32))
+        place(nc.scalar, 0, got2[:, 0:S2].bitcast(I32))
 
 
         v_all = late.tile([P, 2 * S], U32, name="v_all", offset=V_ALL, align_bytes=64)
@@ -173,35 +168,56 @@ def tile_list_expert_patch_energies_kernel(
                     w_w[:, N * g : N * (g + 1)].bitcast(FP8X4), w_sc[:, N * g : N * (g + 1)], w_bf[g][:]
                 )
 
-        def responses(j0, width, groups):
-            h, jh = divmod(j0, 512)
-            units = [(g, c0) for g in groups for c0 in range(0, width, P)]
-            banks = [psum.tile([P, BANK], F32, name="bank", tag="a_bank") for unit in units]
+        units = [(0, 256, (0,)), (0, 256, (1,)), (256, 256, (0, 1)), (512, 256, (0, 1)),
+                 (768, P, (0, 1)), (896, P, (0,)), (896, P, (1,))]
+        blocks = [(g, j0 + c0) for j0, width, groups in units for g in groups for c0 in range(0, width, P)]
+        banks = []
+
+        def responses(count):
+            first = len(banks)
+            new = blocks[first : first + count]
+            banks.extend(psum.tile([P, BANK], F32, name="bank", tag="a_bank") for block in new)
             for a in range(2):
-                for (g, c0), bank in zip(units, banks):
+                for (g, j0), bank in zip(new, banks[first:]):
+                    h, jh = divmod(j0, 512)
                     for t in range(PACK):
                         i0 = S * a + PASS * g + P * t
                         nc.tensor.matmul_mx(
                             bank[:, P * t : P * (t + 1)],
                             lhsT=v_w[a, g][:, P * t : P * (t + 1)].bitcast(FP8X4),
-                            lhsT_scale=v_sc[:, i0 : i0 + P],
-                            rhs=v2_w[a, h][:, jh + c0 : jh + c0 + P].bitcast(FP8X4),
-                            rhs_scale=v2_sc[:, S2 * a + j0 + c0 : S2 * a + j0 + c0 + P],
+                            lhsT_scale=v2_sc[4:P, i0 : i0 + P],
+                            rhs=v2_w[a, h][:, jh : jh + P].bitcast(FP8X4),
+                            rhs_scale=v2_sc[:, S2 * a + j0 : S2 * a + j0 + P],
                             start=(a == 0 and t == 0),
                             stop=(a == 1 and t == PACK - 1),
                         )
-            return banks
 
-        def energies(j0, width, groups, banks=None):
+        places = []
+        for n, (j0, width, groups) in enumerate(units):
+            places.extend((n, u) for u in range(width // P * len(groups)))
+        squared = []
+        sq_tiles = {}
+
+        def square():
+            n, u = places[len(squared)]
+            j0, width, groups = units[n]
+            if u == 0:
+                sq_tiles[n] = ring.tile([P, PACK * width * len(groups)], F32, name="sq", align_bytes=64, bufs=2)
+            nc.scalar.activation(
+                sq_tiles[n][:, BANK * u : BANK * (u + 1)].rearrange("p (j t) -> p j t", t=PACK),
+                banks[len(squared)][:].rearrange("p (t j) -> p j t", t=PACK),
+                ACT.Square,
+                bias=zero[:],
+            )
+            squared.append((n, u))
+            responses(1)
+
+        def energies(n):
+            j0, width, groups = units[n]
             cols = PACK * width * len(groups)
-            sq = ring.tile([P, cols], F32, name="sq", align_bytes=64, bufs=2)
-            for u, (g, c0) in enumerate([(g, c0) for g in groups for c0 in range(0, width, P)]):
-                bank = banks[u] if banks else responses(j0 + c0, P, (g,))[0]
-                nc.scalar.activation(
-                    sq[:, BANK * u : BANK * (u + 1)].rearrange("p (j t) -> p j t", t=PACK),
-                    bank[:].rearrange("p (t j) -> p j t", t=PACK),
-                    ACT.Square,
-                )
+            while len(squared) < len(places) and (n + 1, 0) not in squared:
+                square()
+            sq = sq_tiles[n]
             ln = ring.tile([P, cols], F32, name="ln", align_bytes=64)
             nc.scalar.activation(ln[:], sq[:], ACT.Ln, bias=ones[:])
             e_bf = ring.tile([P, cols], BF16, name="e_bf", align_bytes=64, bufs=2)
@@ -275,15 +291,15 @@ def tile_list_expert_patch_energies_kernel(
             nc.sync.dma_start(y_words[:, j0 : j0 + width], y_w[:, j0 : j0 + width].bitcast(I32))
 
         deal_w4()
-        banks = responses(0, 256, (0, 1))
-        made = energies(0, 256, (0,), banks[:2]) + energies(0, 256, (1,), banks[2:])
+        responses(4)
+        made = energies(0) + energies(1)
         quantise_w()
-        made = made + energies(256, 256, (0, 1))
-        third = energies(512, 256, (0, 1))
+        made = made + energies(2)
+        third = energies(3)
         mix(0, 512, made)
-        made = energies(768, 128, (0, 1))
+        made = energies(4)
         mix(512, 256, third)
-        last = energies(896, 128, (0,)) + energies(896, 128, (1,))
+        last = energies(5) + energies(6)
         mix(768, 128, made)
         mix(896, 128, last)
         for q in range(4):

@@ -113,10 +113,11 @@ def tile_list_expert_patch_energies_kernel(
                     v_w[a, g].rearrange("p (t b r) -> p b t r", t=PACK, r=8),
                     filt[:, a * T : (a + 1) * T].bitcast(U32).indirect(list1[:, 32 * g : 32 * (g + 1)]),
                 )
-        for a in range(2):
-            for h in range(2):
+        for a, cuts in enumerate(((0, 512, 1024), (0, 256, 512, 1024))):
+            for j0, j1 in zip(cuts, cuts[1:]):
                 nc.vector.tensor_copy(
-                    v2_w[a, h], patch[a][:].bitcast(U32).indirect(list2[:, 32 * h : 32 * (h + 1)])
+                    v2_all[:, S2 * a + j0 : S2 * a + j1],
+                    patch[a][:].bitcast(U32).indirect(list2[:, j0 // 16 : j1 // 16]),
                 )
 
         w4_sc_raw = late.tile([P, 2 * N], U8, name="w4_sc_raw", offset=W4_SC_RAW)
@@ -219,18 +220,27 @@ def tile_list_expert_patch_energies_kernel(
                 square()
             sq = sq_tiles[n]
             ln = ring.tile([P, cols], F32, name="ln", align_bytes=64)
-            nc.scalar.activation(ln[:], sq[:], ACT.Ln, bias=ones[:])
+            cut = cols // 2 if n == len(units) - 1 or cols > 2 * BANK else cols
+            for c0 in range(0, cols, cut):
+                nc.scalar.activation(ln[:, c0 : c0 + cut], sq[:, c0 : c0 + cut], ACT.Ln, bias=ones[:])
             e_bf = ring.tile([P, cols], BF16, name="e_bf", align_bytes=64, bufs=2)
             gains = alpha_col[:, PACK * groups[0] : PACK * (groups[-1] + 1)].rearrange("p (g t) -> p g t", t=PACK)
-            nc.vector.tensor_tensor(
-                e_bf[:].rearrange("p (g j t) -> p g j t", g=len(groups), t=PACK),
-                ln[:].rearrange("p (g j t) -> p g j t", g=len(groups), t=PACK),
-                gains.unsqueeze(2).to_broadcast([P, len(groups), width, PACK]),
-                MULT,
-            )
+            half = cols // 2
+            for u in range(2):
+                nc.vector.tensor_tensor(
+                    e_bf[:, half * u : half * (u + 1)].rearrange("p (j t) -> p j t", t=PACK),
+                    ln[:, half * u : half * (u + 1)].rearrange("p (j t) -> p j t", t=PACK),
+                    gains[:, u * len(groups) // 2, :].unsqueeze(1).to_broadcast([P, half // PACK, PACK]),
+                    MULT,
+                )
             e_w = ring.tile([P, cols // PACK], U32, name="e_w", align_bytes=64, bufs=5)
             e_sc = ring.tile([P, cols // PACK], U8, name="e_sc", align_bytes=64, bufs=5)
-            nc.vector.quantize_mx(e_w[:].bitcast(FP8X4), e_sc[:], e_bf[:])
+            words = half // PACK
+            for u in range(2):
+                nc.vector.quantize_mx(
+                    e_w[:, words * u : words * (u + 1)].bitcast(FP8X4), e_sc[:, words * u : words * (u + 1)],
+                    e_bf[:, half * u : half * (u + 1)],
+                )
             return [
                 (j0, width, g, e_w[:, width * u : width * (u + 1)], e_sc[:, width * u : width * (u + 1)])
                 for u, g in enumerate(groups)
@@ -283,11 +293,17 @@ def tile_list_expert_patch_energies_kernel(
                     )
             nc.sync.dma_start(y_rows[:, :, j0 : j0 + width], y[:])
             y_bf = ring.tile([P, PACK * width], BF16, name="y_bf", align_bytes=64)
-            nc.vector.tensor_copy(
-                y_bf[:].rearrange("p (c i t) -> p c t i", t=PACK, i=4),
-                y[:].rearrange("p t (c i) -> p c t i", i=4),
-            )
-            nc.vector.quantize_mx(y_w[:, j0 : j0 + width].bitcast(FP8X4), y_sc[:, j0 : j0 + width], y_bf[:])
+            half = width // 2
+            for c0 in (0, half):
+                nc.vector.tensor_copy(
+                    y_bf[:, PACK * c0 : PACK * (c0 + half)].rearrange("p (c i t) -> p c t i", t=PACK, i=4),
+                    y[:, :, c0 : c0 + half].rearrange("p t (c i) -> p c t i", i=4),
+                )
+            for c0 in (0, half):
+                nc.vector.quantize_mx(
+                    y_w[:, j0 + c0 : j0 + c0 + half].bitcast(FP8X4), y_sc[:, j0 + c0 : j0 + c0 + half],
+                    y_bf[:, PACK * c0 : PACK * (c0 + half)],
+                )
             nc.sync.dma_start(y_words[:, j0 : j0 + width], y_w[:, j0 : j0 + width].bitcast(I32))
 
         deal_w4()

@@ -169,8 +169,8 @@ def tile_list_expert_patch_energies_kernel(
                     w_w[:, N * g : N * (g + 1)].bitcast(FP8X4), w_sc[:, N * g : N * (g + 1)], w_bf[g][:]
                 )
 
-        units = [(0, 256, (0,)), (0, 256, (1,)), (256, 256, (0, 1)), (512, 256, (0, 1)),
-                 (768, P, (0, 1)), (896, P, (0,)), (896, P, (1,))]
+        units = [(j0, 256, (g,)) for j0 in (0, 256, 512) for g in range(2)]
+        units = units + [(768, P, (0, 1)), (896, P, (0,)), (896, P, (1,))]
         blocks = [(g, j0 + c0) for j0, width, groups in units for g in groups for c0 in range(0, width, P)]
         banks = []
 
@@ -233,8 +233,8 @@ def tile_list_expert_patch_energies_kernel(
                     gains[:, u * len(groups) // 2, :].unsqueeze(1).to_broadcast([P, half // PACK, PACK]),
                     MULT,
                 )
-            e_w = ring.tile([P, cols // PACK], U32, name="e_w", align_bytes=64, bufs=5)
-            e_sc = ring.tile([P, cols // PACK], U8, name="e_sc", align_bytes=64, bufs=5)
+            e_w = ring.tile([P, cols // PACK], U32, name="e_w", align_bytes=64, bufs=7)
+            e_sc = ring.tile([P, cols // PACK], U8, name="e_sc", align_bytes=64, bufs=7)
             words = half // PACK
             for u in range(2):
                 nc.vector.quantize_mx(
@@ -251,25 +251,23 @@ def tile_list_expert_patch_energies_kernel(
         y_rows = out_0.rearrange("(p t) j -> p t j", t=PACK)
         y_words = out_1[0].rearrange("p m t -> p (m t)").bitcast(I32)
 
-        def mix(j0, width, made):
+        def mix(j0, width, made, on_vector):
             h, jh = divmod(j0, 512)
             per_bank = BANK // width
-            step = BANK if width == BANK else P
             y = ring.tile([P, PACK, width], F32, name="y", align_bytes=64)
             for t0 in range(0, PACK, per_bank):
-                bank = psum.tile([P, BANK], F32, name="y_bank", tag="y_bank")
+                bank = psum.tile([P, BANK], F32, name="y_bank", tag="y_bank" if width > P else "a_bank")
                 passes = []
                 for t in range(t0, t0 + per_bank):
                     for a in range(2):
                         n0 = N * a + P * t
-                        for c0 in range(0, width, step):
-                            passes.append((
-                                bank[:, width * (t - t0) + c0 : width * (t - t0) + c0 + step],
-                                w4_w[:, n0 : n0 + P].bitcast(U8).bitcast(FP4X4),
-                                w4_sc[:, n0 : n0 + P],
-                                v2_w[a, h][:, jh + c0 : jh + c0 + step].bitcast(FP8X4),
-                                v2_sc[:, S2 * a + j0 + c0 : S2 * a + j0 + c0 + step],
-                            ))
+                        passes.append((
+                            bank[:, width * (t - t0) : width * (t - t0 + 1)],
+                            w4_w[:, n0 : n0 + P].bitcast(U8).bitcast(FP4X4),
+                            w4_sc[:, n0 : n0 + P],
+                            v2_w[a, h][:, jh : jh + width].bitcast(FP8X4),
+                            v2_sc[:, S2 * a + j0 : S2 * a + j0 + width],
+                        ))
                 for je, we, g, e_w, e_sc in made:
                     for t in range(t0, t0 + per_bank):
                         n0 = N * g + P * t
@@ -286,6 +284,14 @@ def tile_list_expert_patch_energies_kernel(
                         dst, lhsT=lhs, lhsT_scale=lhs_sc, rhs=rhs, rhs_scale=rhs_sc,
                         start=(n == 0), stop=(n == len(passes) - 1),
                     )
+                if t0 in on_vector:
+                    nc.vector.tensor_tensor(
+                        y[:, t0 : t0 + per_bank, :],
+                        bank[:].rearrange("p (t j) -> p t j", j=width),
+                        bias[:, t0 : t0 + per_bank].unsqueeze(2).to_broadcast([P, per_bank, width]),
+                        ADD,
+                    )
+                    continue
                 for t in range(t0, t0 + per_bank):
                     nc.scalar.activation(
                         y[:, t, :], bank[:, width * (t - t0) : width * (t - t0 + 1)], ACT.Identity,
@@ -304,20 +310,27 @@ def tile_list_expert_patch_energies_kernel(
                     y_w[:, j0 + c0 : j0 + c0 + half].bitcast(FP8X4), y_sc[:, j0 + c0 : j0 + c0 + half],
                     y_bf[:, PACK * c0 : PACK * (c0 + half)],
                 )
-            nc.sync.dma_start(y_words[:, j0 : j0 + width], y_w[:, j0 : j0 + width].bitcast(I32))
+
+        def store_words(j0, j1):
+            nc.sync.dma_start(y_words[:, j0:j1], y_w[:, j0:j1].bitcast(I32))
 
         deal_w4()
         responses(4)
         made = energies(0) + energies(1)
         quantise_w()
-        made = made + energies(2)
-        third = energies(3)
-        mix(0, 512, made)
-        made = energies(4)
-        mix(512, 256, third)
-        last = energies(5) + energies(6)
-        mix(768, 128, made)
-        mix(896, 128, last)
+        second = energies(2) + energies(3)
+        mix(0, 256, made, (2,))
+        third = energies(4)
+        mix(256, 256, second, (2,))
+        store_words(0, 512)
+        third = third + energies(5)
+        made = energies(6)
+        mix(512, 256, third, ())
+        store_words(512, 768)
+        last = energies(7) + energies(8)
+        mix(768, 128, made, ())
+        mix(896, 128, last, ())
+        store_words(768, S2)
         for q in range(4):
             queue = nc.scalar if q % 2 else nc.sync
             queue.dma_start(

@@ -49,12 +49,15 @@ def tile_list_expert_patch_energies_kernel(
         nc.sync.dma_start(win1[ROW0:P, :].bitcast(I32), tab_scales.rearrange("a q n -> q a n").bitcast(I32))
         nc.sync.dma_start(list2[:], offs2)
         nc.sync.dma_start(win2[ROW0:P, :].bitcast(I32), tab2_scales.rearrange("a q n -> q a n").bitcast(I32))
+        w4_sc_raw = keep.tile([P, N], U8, name="w4_sc_raw")
+        nc.sync.dma_start(w4_sc_raw[ROW0:P, :].bitcast(I32), w4_scales.rearrange("a q n -> q a n").bitcast(I32))
         ones = keep.tile([P, 1], F32, name="ones")
         nc.vector.memset(ones[:], 1.0)
         rows = keep.tile([P, P], F32, name="rows")
         nc.vector.memset(rows[:], 0.0)
         nc.vector.memset(win1[0:ROW0, :].bitcast(I32), 0)
         nc.vector.memset(win2[0:ROW0, :].bitcast(I32), 0)
+        nc.vector.memset(w4_sc_raw[0:ROW0, :].bitcast(I32), 0)
         zero = keep.tile([P, 1], F32, name="zero")
         nc.scalar.activation(zero[:], ones[:], ACT.Ln)
 
@@ -83,10 +86,10 @@ def tile_list_expert_patch_energies_kernel(
         alpha_col = keep.tile([P, 2 * PACK], F32, name="alpha_col")
         nc.scalar.copy(alpha_col[:], turned[:, 0 : 2 * PACK])
 
-        def place(queue, row, picked):
+        def place(queue, planes, row, picked):
             for q in (0, 2, 1, 3):
                 queue.dma_start(
-                    v2_sc[32 * q + row : 32 * q + row + 4, :].bitcast(I32).rearrange("r (a n) -> r a n", a=2),
+                    planes[32 * q + row : 32 * q + row + 4, :].bitcast(I32).rearrange("r (a n) -> r a n", a=2),
                     picked[ROW0 + 8 * q : ROW0 + 8 * (q + 1), :],
                 )
 
@@ -97,10 +100,10 @@ def tile_list_expert_patch_energies_kernel(
             dealt1[:].rearrange("p (g t b r) -> p g t b r", g=2, t=PACK, r=2),
             got1[:].bitcast(I32).rearrange("p (g b t r) -> p g t b r", g=2, t=PACK, r=2),
         )
-        place(nc.gpsimd, 4, dealt1)
+        place(nc.gpsimd, v2_sc, 4, dealt1)
         got2 = late.tile([P, W4_SC_RAW + 2 * N - LATE], U8, name="got2", offset=LATE)
         nc.vector.tensor_copy(got2[:, 0:S2], win2[:].indirect(list2[:]))
-        place(nc.scalar, 0, got2[:, 0:S2].bitcast(I32))
+        place(nc.scalar, v2_sc, 0, got2[:, 0:S2].bitcast(I32))
 
 
         v_all = late.tile([P, 2 * S], U32, name="v_all", offset=V_ALL, align_bytes=64)
@@ -120,18 +123,19 @@ def tile_list_expert_patch_energies_kernel(
                     patch[a][:].bitcast(U32).indirect(list2[:, j0 // 16 : j1 // 16]),
                 )
 
-        w4_sc_raw = late.tile([P, 2 * N], U8, name="w4_sc_raw", offset=W4_SC_RAW)
-        nc.gpsimd.memset(w4_sc_raw[:].bitcast(I32), 0)
-        for q in range(4):
-            nc.sync.dma_start(
-                w4_sc_raw[32 * q : 32 * q + 4, :].bitcast(I32).rearrange("r (a n) -> r a n", a=2),
-                w4_scales[:, 4 * q : 4 * q + 4, :].rearrange("a r n -> r a n").bitcast(I32),
-            )
         w4_raw = late.tile([P, 2 * N], U16, name="w4_raw", offset=W4_RAW)
         nc.sync.dma_start(
             w4_raw[:].bitcast(I32).rearrange("p (a n) -> p a n", a=2),
             w4_words.rearrange("a p n -> p a n").bitcast(I32),
         )
+        w4_sc_dealt = keep.tile([P, N], U8, name="w4_sc_dealt")
+        nc.vector.tensor_copy(
+            w4_sc_dealt[:].rearrange("p (t m) -> p t m", t=PACK),
+            w4_sc_raw[:].rearrange("p (m t) -> p t m", t=PACK),
+        )
+        w4_sc = late.tile([P, 2 * N], U8, name="w4_sc", align_bytes=64, offset=W4_SC_RAW)
+        nc.gpsimd.memset(w4_sc[:].bitcast(I32), 0)
+        place(nc.sync, w4_sc, 0, w4_sc_dealt[:].bitcast(I32))
         w_raw = []
         for g in range(2):
             w_raw.append(late.tile([P, PACK, N], F32, name="w_raw%d" % g, offset=LATE + 4 * PACK * N * g))
@@ -140,15 +144,10 @@ def tile_list_expert_patch_energies_kernel(
                 nc.sync.dma_start(w_raw[g][:, t, :], dealt_rows[t])
 
         w4_w = keep.tile([P, 2 * N], U16, name="w4_w", align_bytes=64)
-        w4_sc = keep.tile([P, 2 * N], U8, name="w4_sc", align_bytes=64)
         w_w = keep.tile([P, 2 * N], U32, name="w_w", align_bytes=64)
         w_sc = keep.tile([P, 2 * N], U8, name="w_sc", align_bytes=64)
 
         def deal_w4():
-            nc.vector.tensor_copy(
-                w4_sc[:].rearrange("p (a t m) -> p a t m", a=2, t=PACK),
-                w4_sc_raw[:].rearrange("p (a m t) -> p a t m", a=2, t=PACK),
-            )
             nc.vector.tensor_copy(
                 w4_w[:].rearrange("p (a t m) -> p a t m", a=2, t=PACK),
                 w4_raw[:].rearrange("p (a m t) -> p a t m", a=2, t=PACK),
@@ -251,9 +250,8 @@ def tile_list_expert_patch_energies_kernel(
         y_rows = out_0.rearrange("(p t) j -> p t j", t=PACK)
         y_words = out_1[0].rearrange("p m t -> p (m t)").bitcast(I32)
 
-        def mix(j0, width, made, on_vector):
+        def mix(j0, width, made, on_vector, per_bank):
             h, jh = divmod(j0, 512)
-            per_bank = BANK // width
             y = ring.tile([P, PACK, width], F32, name="y", align_bytes=64)
             for t0 in range(0, PACK, per_bank):
                 bank = psum.tile([P, BANK], F32, name="y_bank", tag="y_bank" if width > P else "a_bank")
@@ -287,7 +285,7 @@ def tile_list_expert_patch_energies_kernel(
                 if t0 in on_vector:
                     nc.vector.tensor_tensor(
                         y[:, t0 : t0 + per_bank, :],
-                        bank[:].rearrange("p (t j) -> p t j", j=width),
+                        bank[:, 0 : per_bank * width].rearrange("p (t j) -> p t j", j=width),
                         bias[:, t0 : t0 + per_bank].unsqueeze(2).to_broadcast([P, per_bank, width]),
                         ADD,
                     )
@@ -298,8 +296,15 @@ def tile_list_expert_patch_energies_kernel(
                         bias=bias[:, t : t + 1],
                     )
             nc.sync.dma_start(y_rows[:, :, j0 : j0 + width], y[:])
+            return y
+
+        def planes(j0, width, y, on_scalar):
             y_bf = ring.tile([P, PACK * width], BF16, name="y_bf", align_bytes=64)
             half = width // 2
+            if on_scalar:
+                nc.scalar.copy(y_bf[:].rearrange("p (j t) -> p j t", t=PACK), y[:].rearrange("p t j -> p j t"))
+                nc.vector.quantize_mx(y_w[:, j0 : j0 + width].bitcast(FP8X4), y_sc[:, j0 : j0 + width], y_bf[:])
+                return
             for c0 in (0, half):
                 nc.vector.tensor_copy(
                     y_bf[:, PACK * c0 : PACK * (c0 + half)].rearrange("p (c i t) -> p c t i", t=PACK, i=4),
@@ -319,17 +324,18 @@ def tile_list_expert_patch_energies_kernel(
         made = energies(0) + energies(1)
         quantise_w()
         second = energies(2) + energies(3)
-        mix(0, 256, made, (2,))
+        planes(0, 256, mix(0, 256, made, (2,), 2), False)
         third = energies(4)
-        mix(256, 256, second, (2,))
+        planes(256, 256, mix(256, 256, second, (2,), 2), False)
         store_words(0, 512)
         third = third + energies(5)
         made = energies(6)
-        mix(512, 256, third, ())
-        store_words(512, 768)
+        y2 = mix(512, 256, third, (), 2)
         last = energies(7) + energies(8)
-        mix(768, 128, made, ())
-        mix(896, 128, last, ())
+        planes(512, 256, y2, False)
+        store_words(512, 768)
+        planes(768, 128, mix(768, 128, made, (), 4), True)
+        planes(896, 128, mix(896, 128, last, (2,), 2), False)
         store_words(768, S2)
         for q in range(4):
             queue = nc.scalar if q % 2 else nc.sync

@@ -1,7 +1,6 @@
 from contextlib import ExitStack
 
 import concourse.mybir as mybir
-from concourse.masks import make_identity
 
 K, T, S, T2, S2, N = 1024, 2048, 1024, 4096, 1024, 512
 FLOPS = 2 * K * S * S2 + 2 * S * N * S2 + 2 * K * N * S2
@@ -23,11 +22,9 @@ PACK = 4
 PASS = 512
 BANK = 512
 ROW0 = 96
-V_ALL = 0
-PATCH1 = V_ALL + 4 * 2 * S
-LATE = PATCH1 + 4 * T2
-W4_RAW = LATE + 4 * 2 * PACK * N
-W4_SC_RAW = W4_RAW + 2 * 2 * N
+WIDE = 256
+W_RAW = T2
+W_HALF = 4 * PACK * N
 
 
 def tile_list_expert_patch_energies_kernel(
@@ -44,76 +41,67 @@ def tile_list_expert_patch_energies_kernel(
         list1 = keep.tile([P, S // 16], U16, name="list1")
         list2 = keep.tile([P, S2 // 16], U16, name="list2")
         win1 = keep.tile([P, T], U8, name="win1")
-        win2 = late.tile([P, T2], U8, name="win2", offset=V_ALL)
+        win2 = late.tile([P, T2], U8, name="win2", offset=0)
         nc.sync.dma_start(list1[:], offs)
         nc.sync.dma_start(win1[ROW0:P, :].bitcast(I32), tab_scales.rearrange("a q n -> q a n").bitcast(I32))
         nc.sync.dma_start(list2[:], offs2)
         nc.sync.dma_start(win2[ROW0:P, :].bitcast(I32), tab2_scales.rearrange("a q n -> q a n").bitcast(I32))
         w4_sc_raw = keep.tile([P, N], U8, name="w4_sc_raw")
         nc.sync.dma_start(w4_sc_raw[ROW0:P, :].bitcast(I32), w4_scales.rearrange("a q n -> q a n").bitcast(I32))
-        ones = keep.tile([P, 1], F32, name="ones")
-        nc.vector.memset(ones[:], 1.0)
-        rows = keep.tile([P, P], F32, name="rows")
-        nc.vector.memset(rows[:], 0.0)
-        nc.vector.memset(win1[0:ROW0, :].bitcast(I32), 0)
-        nc.vector.memset(win2[0:ROW0, :].bitcast(I32), 0)
-        nc.vector.memset(w4_sc_raw[0:ROW0, :].bitcast(I32), 0)
-        zero = keep.tile([P, 1], F32, name="zero")
-        nc.scalar.activation(zero[:], ones[:], ACT.Ln)
-
         filt = keep.tile([P, 2 * T], I32, name="filt")
         nc.sync.dma_start(
             filt[:].rearrange("p (a n) -> p a n", a=2),
             tab_words.rearrange("a p n i -> p a (n i)").bitcast(I32),
         )
-        patch = [keep.tile([P, T2], I32, name="patch0"), late.tile([P, T2], I32, name="patch1", offset=PATCH1)]
+        patch = [keep.tile([P, T2], I32, name="patch%d" % a) for a in range(2)]
         for a in range(2):
             nc.sync.dma_start(patch[a][:], tab2_words[a].rearrange("p n i -> p (n i)").bitcast(I32))
+        gains = keep.tile([P, 2, 2 * PACK], F32, name="gains")
+        nc.sync.dma_start(gains[:, :, 0:PACK], alpha.rearrange("(g p t) -> p g t", g=2, t=PACK))
 
-        v2_sc = keep.tile([P, 2 * S2], U8, name="v2_sc", align_bytes=64)
-        ident = keep.tile([P, P], F32, name="ident")
-        nc.vector.memset(v2_sc[:].bitcast(I32), 0)
-        make_identity(nc, ident[:])
-        for g in range(2):
-            nc.scalar.dma_start(
-                rows[PACK * g : PACK * (g + 1), :].rearrange("t (b r) -> t b r", r=8),
-                alpha[PASS * g : PASS * (g + 1)].rearrange("(b t r) -> t b r", t=PACK, r=8),
-            )
+        ones = keep.tile([P, 1], F32, name="ones")
+        nc.vector.memset(ones[:], 1.0)
+        nc.vector.memset(win1[0:ROW0, :].bitcast(I32), 0)
+        nc.vector.memset(win2[0:ROW0, :].bitcast(I32), 0)
+        v_sc = keep.tile([P, 2 * S2], U8, name="v_sc", align_bytes=64)
+        nc.vector.memset(v_sc[:].bitcast(I32), 0)
+        zero = keep.tile([P, 1], F32, name="zero")
+        nc.scalar.activation(zero[:], ones[:], ACT.Ln)
+
+        w4_sc = keep.tile([P, 2 * N], U8, name="w4_sc", align_bytes=64)
+        nc.vector.memset(w4_sc_raw[0:ROW0, :].bitcast(I32), 0)
+        nc.vector.memset(w4_sc[:].bitcast(I32), 0)
         bias = keep.tile([P, PACK], F32, name="bias")
         nc.gpsimd.dma_start(bias[:], b.rearrange("(p t) -> p t", t=PACK))
-        turned = psum.tile([P, BANK], F32, name="turned", tag="a_bank")
-        nc.tensor.transpose(turned[:, 0:P], rows[:], ident[:])
-        alpha_col = keep.tile([P, 2 * PACK], F32, name="alpha_col")
-        nc.scalar.copy(alpha_col[:], turned[:, 0 : 2 * PACK])
 
         def place(queue, planes, row, picked):
             for q in (0, 2, 1, 3):
                 queue.dma_start(
                     planes[32 * q + row : 32 * q + row + 4, :].bitcast(I32).rearrange("r (a n) -> r a n", a=2),
-                    picked[ROW0 + 8 * q : ROW0 + 8 * (q + 1), :],
+                    picked[ROW0 + 8 * q : ROW0 + 8 * (q + 1), :].bitcast(I32),
                 )
 
         got1 = keep.tile([P, S], U8, name="got1")
-        nc.vector.tensor_copy(got1[:], win1[:].indirect(list1[:]))
-        dealt1 = keep.tile([P, S // 4], I32, name="dealt1")
         nc.vector.tensor_copy(
-            dealt1[:].rearrange("p (g t b r) -> p g t b r", g=2, t=PACK, r=2),
-            got1[:].bitcast(I32).rearrange("p (g b t r) -> p g t b r", g=2, t=PACK, r=2),
+            got1[:].rearrange("p (g t m) -> p g m t", g=2, t=PACK), win1[:].indirect(list1[:])
         )
-        place(nc.gpsimd, v2_sc, 4, dealt1)
-        got2 = late.tile([P, W4_SC_RAW + 2 * N - LATE], U8, name="got2", offset=LATE)
-        nc.vector.tensor_copy(got2[:, 0:S2], win2[:].indirect(list2[:]))
-        place(nc.scalar, v2_sc, 0, got2[:, 0:S2].bitcast(I32))
+        place(nc.gpsimd, v_sc, 4, got1)
+        got2 = late.tile([P, S2], U8, name="got2", offset=W_RAW + W_HALF - S2 // 2)
+        nc.vector.tensor_copy(got2[:], win2[:].indirect(list2[:]))
+        place(nc.scalar, v_sc, 0, got2)
+        w4_sc_dealt = keep.tile([P, N], U8, name="w4_sc_dealt")
+        nc.vector.tensor_copy(
+            w4_sc_dealt[:].rearrange("p (t m) -> p m t", t=PACK),
+            w4_sc_raw[:].rearrange("p (m t) -> p m t", t=PACK),
+        )
+        place(nc.gpsimd, w4_sc, 0, w4_sc_dealt)
 
-
-        v_all = late.tile([P, 2 * S], U32, name="v_all", offset=V_ALL, align_bytes=64)
+        v_all = keep.tile([P, 2 * S], U32, name="v_all", align_bytes=64)
         v2_all = keep.tile([P, 2 * S2], U32, name="v2_all", align_bytes=64)
-        v_w = {(a, g): v_all[:, S * a + PASS * g : S * a + PASS * (g + 1)] for a in range(2) for g in range(2)}
-        v2_w = {(a, h): v2_all[:, S2 * a + 512 * h : S2 * a + 512 * (h + 1)] for a in range(2) for h in range(2)}
         for g in range(2):
             for a in range(2):
                 nc.vector.tensor_copy(
-                    v_w[a, g].rearrange("p (t b r) -> p b t r", t=PACK, r=8),
+                    v_all[:, S * a + PASS * g : S * a + PASS * (g + 1)].rearrange("p (t m) -> p m t", t=PACK),
                     filt[:, a * T : (a + 1) * T].bitcast(U32).indirect(list1[:, 32 * g : 32 * (g + 1)]),
                 )
         for a, cuts in enumerate(((0, 512, 1024), (0, 256, 512, 1024))):
@@ -123,54 +111,46 @@ def tile_list_expert_patch_energies_kernel(
                     patch[a][:].bitcast(U32).indirect(list2[:, j0 // 16 : j1 // 16]),
                 )
 
-        w4_raw = late.tile([P, 2 * N], U16, name="w4_raw", offset=W4_RAW)
+        w4_raw = late.tile([P, 2 * N], U16, name="w4_raw", offset=0)
         nc.sync.dma_start(
             w4_raw[:].bitcast(I32).rearrange("p (a n) -> p a n", a=2),
             w4_words.rearrange("a p n -> p a n").bitcast(I32),
         )
-        w4_sc_dealt = keep.tile([P, N], U8, name="w4_sc_dealt")
-        nc.vector.tensor_copy(
-            w4_sc_dealt[:].rearrange("p (t m) -> p t m", t=PACK),
-            w4_sc_raw[:].rearrange("p (m t) -> p t m", t=PACK),
-        )
-        w4_sc = late.tile([P, 2 * N], U8, name="w4_sc", align_bytes=64, offset=W4_SC_RAW)
-        nc.gpsimd.memset(w4_sc[:].bitcast(I32), 0)
-        place(nc.sync, w4_sc, 0, w4_sc_dealt[:].bitcast(I32))
         w_raw = []
         for g in range(2):
-            w_raw.append(late.tile([P, PACK, N], F32, name="w_raw%d" % g, offset=LATE + 4 * PACK * N * g))
-            dealt_rows = w[PASS * g : PASS * (g + 1), :].rearrange("(b t r) n -> t b r n", t=PACK, r=8)
-            for t in range(PACK):
-                nc.sync.dma_start(w_raw[g][:, t, :], dealt_rows[t])
+            w_raw.append(late.tile([P, PACK * N], F32, name="w_raw%d" % g, offset=W_RAW + W_HALF * g))
+            nc.sync.dma_start(
+                w_raw[g][:], w[PASS * g : PASS * (g + 1), :].rearrange("(p s) n -> p (s n)", s=PACK)
+            )
 
         w4_w = keep.tile([P, 2 * N], U16, name="w4_w", align_bytes=64)
         w_w = keep.tile([P, 2 * N], U32, name="w_w", align_bytes=64)
         w_sc = keep.tile([P, 2 * N], U8, name="w_sc", align_bytes=64)
+        w_bf = [keep.tile([P, PACK * N], BF16, name="w_bf%d" % g, align_bytes=64) for g in range(2)]
 
         def deal_w4():
             nc.vector.tensor_copy(
-                w4_w[:].rearrange("p (a t m) -> p a t m", a=2, t=PACK),
-                w4_raw[:].rearrange("p (a m t) -> p a t m", a=2, t=PACK),
+                w4_w[:].rearrange("p (a t m) -> p a m t", a=2, t=PACK),
+                w4_raw[:].rearrange("p (a m t) -> p a m t", a=2, t=PACK),
             )
 
-        def quantise_w():
-            w_bf = []
-            for g in range(2):
-                w_bf.append(late.tile(
-                    [P, PACK * N], BF16, name="w_bf%d" % g, align_bytes=64, offset=PATCH1 + 2 * PACK * N * g
-                ))
-                nc.vector.tensor_copy(
-                    w_bf[g][:].rearrange("p (t m s) -> p m t s", t=PACK, s=PACK),
-                    w_raw[g][:].rearrange("p s (m t) -> p m t s", t=PACK),
-                )
-            for g in range(2):
-                nc.vector.quantize_mx(
-                    w_w[:, N * g : N * (g + 1)].bitcast(FP8X4), w_sc[:, N * g : N * (g + 1)], w_bf[g][:]
-                )
+        def round_w(g):
+            nc.vector.tensor_copy(
+                w_bf[g][:].rearrange("p (t m s) -> p m s t", t=PACK, s=PACK),
+                w_raw[g][:].rearrange("p (s m t) -> p m s t", s=PACK, t=PACK),
+            )
 
-        units = [(j0, 256, (g,)) for j0 in (0, 256, 512) for g in range(2)]
+        def quantise_w(g):
+            nc.vector.quantize_mx(
+                w_w[:, N * g : N * (g + 1)].bitcast(FP8X4), w_sc[:, N * g : N * (g + 1)], w_bf[g][:]
+            )
+
+        units = [(j0, WIDE, (g,)) for j0 in (0, 256, 512) for g in range(2)]
         units = units + [(768, P, (0, 1)), (896, P, (0,)), (896, P, (1,))]
-        blocks = [(g, j0 + c0) for j0, width, groups in units for g in groups for c0 in range(0, width, P)]
+        blocks = []
+        for n, (j0, width, groups) in enumerate(units):
+            per_bank = BANK // width
+            blocks.extend((n, g, j0, width, t0) for g in groups for t0 in range(0, PACK, per_bank))
         banks = []
 
         def responses(count):
@@ -178,63 +158,64 @@ def tile_list_expert_patch_energies_kernel(
             new = blocks[first : first + count]
             banks.extend(psum.tile([P, BANK], F32, name="bank", tag="a_bank") for block in new)
             for a in range(2):
-                for (g, j0), bank in zip(new, banks[first:]):
-                    h, jh = divmod(j0, 512)
-                    for t in range(PACK):
-                        i0 = S * a + PASS * g + P * t
+                for (n, g, j0, width, t0), bank in zip(new, banks[first:]):
+                    per_bank = BANK // width
+                    for u in range(per_bank):
+                        i0 = S * a + PASS * g + P * (t0 + u)
                         nc.tensor.matmul_mx(
-                            bank[:, P * t : P * (t + 1)],
-                            lhsT=v_w[a, g][:, P * t : P * (t + 1)].bitcast(FP8X4),
-                            lhsT_scale=v2_sc[4:P, i0 : i0 + P],
-                            rhs=v2_w[a, h][:, jh : jh + P].bitcast(FP8X4),
-                            rhs_scale=v2_sc[:, S2 * a + j0 : S2 * a + j0 + P],
-                            start=(a == 0 and t == 0),
-                            stop=(a == 1 and t == PACK - 1),
+                            bank[:, width * u : width * (u + 1)],
+                            lhsT=v_all[:, i0 : i0 + P].bitcast(FP8X4),
+                            lhsT_scale=v_sc[4:P, i0 : i0 + P],
+                            rhs=v2_all[:, S2 * a + j0 : S2 * a + j0 + width].bitcast(FP8X4),
+                            rhs_scale=v_sc[:, S2 * a + j0 : S2 * a + j0 + width],
+                            start=(a == 0 and u == 0),
+                            stop=(a == 1 and u == per_bank - 1),
                         )
 
-        places = []
-        for n, (j0, width, groups) in enumerate(units):
-            places.extend((n, u) for u in range(width // P * len(groups)))
         squared = []
         sq_tiles = {}
 
         def square():
-            n, u = places[len(squared)]
-            j0, width, groups = units[n]
+            n, g, j0, width, t0 = blocks[len(squared)]
+            u = squared.count(n)
             if u == 0:
-                sq_tiles[n] = ring.tile([P, PACK * width * len(groups)], F32, name="sq", align_bytes=64, bufs=2)
+                sq_tiles[n] = ring.tile([P, PACK * width * len(units[n][2])], F32, name="sq", align_bytes=64, bufs=2)
             nc.scalar.activation(
-                sq_tiles[n][:, BANK * u : BANK * (u + 1)].rearrange("p (j t) -> p j t", t=PACK),
-                banks[len(squared)][:].rearrange("p (t j) -> p j t", t=PACK),
+                sq_tiles[n][:, BANK * u : BANK * (u + 1)].rearrange("p (j t) -> p j t", j=width),
+                banks[len(squared)][:].rearrange("p (t j) -> p j t", j=width),
                 ACT.Square,
                 bias=zero[:],
             )
-            squared.append((n, u))
+            squared.append(n)
             responses(1)
 
         def energies(n):
             j0, width, groups = units[n]
             cols = PACK * width * len(groups)
-            while len(squared) < len(places) and (n + 1, 0) not in squared:
+            while len(squared) < len(blocks) and n + 1 not in squared:
                 square()
             sq = sq_tiles[n]
-            ln = ring.tile([P, cols], F32, name="ln", align_bytes=64)
-            cut = cols // 2 if n == len(units) - 1 or cols > 2 * BANK else cols
+            ln = ring.tile([P, cols], F32, name="ln", align_bytes=64, bufs=4)
+            cut = cols // 2 if n == len(units) - 1 else cols
             for c0 in range(0, cols, cut):
                 nc.scalar.activation(ln[:, c0 : c0 + cut], sq[:, c0 : c0 + cut], ACT.Ln, bias=ones[:])
             e_bf = ring.tile([P, cols], BF16, name="e_bf", align_bytes=64, bufs=2)
-            gains = alpha_col[:, PACK * groups[0] : PACK * (groups[-1] + 1)].rearrange("p (g t) -> p g t", t=PACK)
             half = cols // 2
+            words = half // PACK
             for u in range(2):
+                if width == WIDE:
+                    src = ln[:].rearrange("p (h j t) -> p j h t", h=2, t=2)[:, words * u : words * (u + 1)]
+                else:
+                    src = ln[:, half * u : half * (u + 1)].rearrange("p (j h t) -> p j h t", h=2, t=2)
+                gain = gains[:, groups[u * len(groups) // 2], 0:PACK].rearrange("p (h t) -> p h t", h=2)
                 nc.vector.tensor_tensor(
-                    e_bf[:, half * u : half * (u + 1)].rearrange("p (j t) -> p j t", t=PACK),
-                    ln[:, half * u : half * (u + 1)].rearrange("p (j t) -> p j t", t=PACK),
-                    gains[:, u * len(groups) // 2, :].unsqueeze(1).to_broadcast([P, half // PACK, PACK]),
+                    e_bf[:, half * u : half * (u + 1)].rearrange("p (j h t) -> p j h t", h=2, t=2),
+                    src,
+                    gain.unsqueeze(1).to_broadcast([P, words, 2, 2]),
                     MULT,
                 )
             e_w = ring.tile([P, cols // PACK], U32, name="e_w", align_bytes=64, bufs=7)
             e_sc = ring.tile([P, cols // PACK], U8, name="e_sc", align_bytes=64, bufs=7)
-            words = half // PACK
             for u in range(2):
                 nc.vector.quantize_mx(
                     e_w[:, words * u : words * (u + 1)].bitcast(FP8X4), e_sc[:, words * u : words * (u + 1)],
@@ -251,7 +232,6 @@ def tile_list_expert_patch_energies_kernel(
         y_words = out_1[0].rearrange("p m t -> p (m t)").bitcast(I32)
 
         def mix(j0, width, made, on_vector, per_bank):
-            h, jh = divmod(j0, 512)
             y = ring.tile([P, PACK, width], F32, name="y", align_bytes=64)
             for t0 in range(0, PACK, per_bank):
                 bank = psum.tile([P, BANK], F32, name="y_bank", tag="y_bank" if width > P else "a_bank")
@@ -263,8 +243,8 @@ def tile_list_expert_patch_energies_kernel(
                             bank[:, width * (t - t0) : width * (t - t0 + 1)],
                             w4_w[:, n0 : n0 + P].bitcast(U8).bitcast(FP4X4),
                             w4_sc[:, n0 : n0 + P],
-                            v2_w[a, h][:, jh : jh + width].bitcast(FP8X4),
-                            v2_sc[:, S2 * a + j0 : S2 * a + j0 + width],
+                            v2_all[:, S2 * a + j0 : S2 * a + j0 + width].bitcast(FP8X4),
+                            v_sc[:, S2 * a + j0 : S2 * a + j0 + width],
                         ))
                 for je, we, g, e_w, e_sc in made:
                     for t in range(t0, t0 + per_bank):
@@ -319,10 +299,14 @@ def tile_list_expert_patch_energies_kernel(
         def store_words(j0, j1):
             nc.sync.dma_start(y_words[:, j0:j1], y_w[:, j0:j1].bitcast(I32))
 
-        deal_w4()
         responses(4)
-        made = energies(0) + energies(1)
-        quantise_w()
+        deal_w4()
+        made = energies(0)
+        round_w(0)
+        made = made + energies(1)
+        round_w(1)
+        quantise_w(0)
+        quantise_w(1)
         second = energies(2) + energies(3)
         planes(0, 256, mix(0, 256, made, (2,), 2), False)
         third = energies(4)

@@ -21,10 +21,13 @@ P = 128
 PACK = 4
 PASS = 512
 BANK = 512
-ROW0 = 96
+ROWS = 32
+LOW, HIGH = 0, 96
 WIDE = 256
-W_RAW = T2
-W_HALF = 4 * PACK * N
+LAP = 32
+GOT2 = 2 * 4 * PACK * N - LAP
+W4_RAW = GOT2 + S2 - LAP
+PATCH0 = W4_RAW + 4 * N
 
 
 def tile_list_expert_patch_energies_kernel(
@@ -41,19 +44,21 @@ def tile_list_expert_patch_energies_kernel(
         list1 = keep.tile([P, S // 16], U16, name="list1")
         list2 = keep.tile([P, S2 // 16], U16, name="list2")
         win1 = keep.tile([P, T], U8, name="win1")
-        win2 = late.tile([P, T2], U8, name="win2", offset=0)
+        win2 = keep.tile([P, T2], U8, name="win2")
         nc.sync.dma_start(list1[:], offs)
-        nc.sync.dma_start(win1[ROW0:P, :].bitcast(I32), tab_scales.rearrange("a q n -> q a n").bitcast(I32))
+        nc.sync.dma_start(win1[LOW : LOW + ROWS, :].bitcast(I32), tab_scales.rearrange("a q n -> q a n").bitcast(I32))
         nc.sync.dma_start(list2[:], offs2)
-        nc.sync.dma_start(win2[ROW0:P, :].bitcast(I32), tab2_scales.rearrange("a q n -> q a n").bitcast(I32))
+        nc.sync.dma_start(win2[HIGH : HIGH + ROWS, :].bitcast(I32), tab2_scales.rearrange("a q n -> q a n").bitcast(I32))
         w4_sc_raw = keep.tile([P, N], U8, name="w4_sc_raw")
-        nc.sync.dma_start(w4_sc_raw[ROW0:P, :].bitcast(I32), w4_scales.rearrange("a q n -> q a n").bitcast(I32))
+        nc.sync.dma_start(
+            w4_sc_raw[LOW : LOW + ROWS, :].bitcast(I32), w4_scales.rearrange("a q n -> q a n").bitcast(I32)
+        )
         filt = keep.tile([P, 2 * T], I32, name="filt")
         nc.sync.dma_start(
             filt[:].rearrange("p (a n) -> p a n", a=2),
             tab_words.rearrange("a p n i -> p a (n i)").bitcast(I32),
         )
-        patch = [keep.tile([P, T2], I32, name="patch%d" % a) for a in range(2)]
+        patch = [late.tile([P, T2], I32, name="patch0", offset=PATCH0), keep.tile([P, T2], I32, name="patch1")]
         for a in range(2):
             nc.sync.dma_start(patch[a][:], tab2_words[a].rearrange("p n i -> p (n i)").bitcast(I32))
         gains = keep.tile([P, 2, 2 * PACK], F32, name="gains")
@@ -61,40 +66,36 @@ def tile_list_expert_patch_energies_kernel(
 
         ones = keep.tile([P, 1], F32, name="ones")
         nc.vector.memset(ones[:], 1.0)
-        nc.vector.memset(win1[0:ROW0, :].bitcast(I32), 0)
-        nc.vector.memset(win2[0:ROW0, :].bitcast(I32), 0)
+        for p0, p1 in ((32, 64), (64, P)):
+            nc.vector.memset(win1[p0:p1, :].bitcast(I32), 0)
+        nc.vector.memset(win2[0:HIGH, :].bitcast(I32), 0)
         v_sc = keep.tile([P, 2 * S2], U8, name="v_sc", align_bytes=64)
         nc.vector.memset(v_sc[:].bitcast(I32), 0)
         zero = keep.tile([P, 1], F32, name="zero")
         nc.scalar.activation(zero[:], ones[:], ACT.Ln)
 
         w4_sc = keep.tile([P, 2 * N], U8, name="w4_sc", align_bytes=64)
-        nc.vector.memset(w4_sc_raw[0:ROW0, :].bitcast(I32), 0)
+        for p0, p1 in ((32, 64), (64, P)):
+            nc.vector.memset(w4_sc_raw[p0:p1, :].bitcast(I32), 0)
         nc.vector.memset(w4_sc[:].bitcast(I32), 0)
         bias = keep.tile([P, PACK], F32, name="bias")
         nc.gpsimd.dma_start(bias[:], b.rearrange("(p t) -> p t", t=PACK))
 
-        def place(queue, planes, row, picked):
+        def place(queue, planes, row, picked, first):
             for q in (0, 2, 1, 3):
                 queue.dma_start(
                     planes[32 * q + row : 32 * q + row + 4, :].bitcast(I32).rearrange("r (a n) -> r a n", a=2),
-                    picked[ROW0 + 8 * q : ROW0 + 8 * (q + 1), :].bitcast(I32),
+                    picked[first + 8 * q : first + 8 * (q + 1), :].bitcast(I32),
                 )
 
         got1 = keep.tile([P, S], U8, name="got1")
         nc.vector.tensor_copy(
             got1[:].rearrange("p (g t m) -> p g m t", g=2, t=PACK), win1[:].indirect(list1[:])
         )
-        place(nc.gpsimd, v_sc, 4, got1)
-        got2 = late.tile([P, S2], U8, name="got2", offset=W_RAW + W_HALF - S2 // 2)
+        place(nc.gpsimd, v_sc, 4, got1, LOW)
+        got2 = late.tile([P, S2], U8, name="got2", offset=GOT2)
         nc.vector.tensor_copy(got2[:], win2[:].indirect(list2[:]))
-        place(nc.scalar, v_sc, 0, got2)
-        w4_sc_dealt = keep.tile([P, N], U8, name="w4_sc_dealt")
-        nc.vector.tensor_copy(
-            w4_sc_dealt[:].rearrange("p (t m) -> p m t", t=PACK),
-            w4_sc_raw[:].rearrange("p (m t) -> p m t", t=PACK),
-        )
-        place(nc.gpsimd, w4_sc, 0, w4_sc_dealt)
+        place(nc.scalar, v_sc, 0, got2, HIGH)
 
         v_all = keep.tile([P, 2 * S], U32, name="v_all", align_bytes=64)
         v2_all = keep.tile([P, 2 * S2], U32, name="v2_all", align_bytes=64)
@@ -111,17 +112,26 @@ def tile_list_expert_patch_energies_kernel(
                     patch[a][:].bitcast(U32).indirect(list2[:, j0 // 16 : j1 // 16]),
                 )
 
-        w4_raw = late.tile([P, 2 * N], U16, name="w4_raw", offset=0)
-        nc.sync.dma_start(
-            w4_raw[:].bitcast(I32).rearrange("p (a n) -> p a n", a=2),
-            w4_words.rearrange("a p n -> p a n").bitcast(I32),
-        )
+        w_all = late.tile([P, 2 * PACK * N], F32, name="w_all", offset=0)
+        w_rows = w.rearrange("(g p s) n -> g p s n", g=2, s=PACK)
+        w_parts = ((0, 0, N // 2), (0, N // 2, N), (1, 0, N))
         w_raw = []
-        for g in range(2):
-            w_raw.append(late.tile([P, PACK * N], F32, name="w_raw%d" % g, offset=W_RAW + W_HALF * g))
-            nc.sync.dma_start(
-                w_raw[g][:], w[PASS * g : PASS * (g + 1), :].rearrange("(p s) n -> p (s n)", s=PACK)
-            )
+        for g, n0, n1 in w_parts:
+            c0 = PACK * (N * g + n0)
+            w_raw.append(w_all[:, c0 : c0 + PACK * (n1 - n0)].rearrange("p (s n) -> p s n", s=PACK))
+            if g == 1:
+                w4_raw = late.tile([P, 2 * N], U16, name="w4_raw", offset=W4_RAW)
+                nc.sync.dma_start(
+                    w4_raw[:].bitcast(I32).rearrange("p (a n) -> p a n", a=2),
+                    w4_words.rearrange("a p n -> p a n").bitcast(I32),
+                )
+            nc.sync.dma_start(w_raw[-1], w_rows[g, :, :, n0:n1])
+        w4_sc_dealt = late.tile([P, N], U8, name="w4_sc_dealt", offset=PATCH0)
+        nc.vector.tensor_copy(
+            w4_sc_dealt[:].rearrange("p (t m) -> p m t", t=PACK),
+            w4_sc_raw[:].rearrange("p (m t) -> p m t", t=PACK),
+        )
+        place(nc.sync, w4_sc, 0, w4_sc_dealt, LOW)
 
         w4_w = keep.tile([P, 2 * N], U16, name="w4_w", align_bytes=64)
         w_w = keep.tile([P, 2 * N], U32, name="w_w", align_bytes=64)
@@ -134,10 +144,11 @@ def tile_list_expert_patch_energies_kernel(
                 w4_raw[:].rearrange("p (a m t) -> p a m t", a=2, t=PACK),
             )
 
-        def round_w(g):
+        def round_w(part):
+            g, n0, n1 = w_parts[part]
             nc.vector.tensor_copy(
-                w_bf[g][:].rearrange("p (t m s) -> p m s t", t=PACK, s=PACK),
-                w_raw[g][:].rearrange("p (s m t) -> p m s t", s=PACK, t=PACK),
+                w_bf[g][:].rearrange("p (t m s) -> p m s t", t=PACK, s=PACK)[:, n0 // PACK : n1 // PACK],
+                w_raw[part].rearrange("p s (m t) -> p m s t", t=PACK),
             )
 
         def quantise_w(g):
@@ -184,7 +195,7 @@ def tile_list_expert_patch_energies_kernel(
                 sq_tiles[n][:, BANK * u : BANK * (u + 1)].rearrange("p (j t) -> p j t", j=width),
                 banks[len(squared)][:].rearrange("p (t j) -> p j t", j=width),
                 ACT.Square,
-                bias=zero[:],
+                bias=0.0 if squared else zero[:],
             )
             squared.append(n)
             responses(1)
@@ -198,7 +209,7 @@ def tile_list_expert_patch_energies_kernel(
             ln = ring.tile([P, cols], F32, name="ln", align_bytes=64, bufs=4)
             cut = cols // 2 if n == len(units) - 1 else cols
             for c0 in range(0, cols, cut):
-                nc.scalar.activation(ln[:, c0 : c0 + cut], sq[:, c0 : c0 + cut], ACT.Ln, bias=ones[:])
+                nc.scalar.activation(ln[:, c0 : c0 + cut], sq[:, c0 : c0 + cut], ACT.Ln, bias=1.0)
             e_bf = ring.tile([P, cols], BF16, name="e_bf", align_bytes=64, bufs=2)
             half = cols // 2
             words = half // PACK
@@ -300,12 +311,13 @@ def tile_list_expert_patch_energies_kernel(
             nc.sync.dma_start(y_words[:, j0:j1], y_w[:, j0:j1].bitcast(I32))
 
         responses(4)
-        deal_w4()
-        made = energies(0)
         round_w(0)
-        made = made + energies(1)
         round_w(1)
+        made = energies(0)
         quantise_w(0)
+        deal_w4()
+        made = made + energies(1)
+        round_w(2)
         quantise_w(1)
         second = energies(2) + energies(3)
         planes(0, 256, mix(0, 256, made, (2,), 2), False)

@@ -164,11 +164,11 @@ def tile_list_expert_patch_energies_kernel(
             blocks.extend((n, g, j0, width, t0) for g in groups for t0 in range(0, PACK, per_bank))
         banks = []
 
-        def responses(count):
+        def responses(count, order=(0, 1)):
             first = len(banks)
             new = blocks[first : first + count]
             banks.extend(psum.tile([P, BANK], F32, name="bank", tag="a_bank") for block in new)
-            for a in range(2):
+            for a in order:
                 for (n, g, j0, width, t0), bank in zip(new, banks[first:]):
                     per_bank = BANK // width
                     for u in range(per_bank):
@@ -179,8 +179,8 @@ def tile_list_expert_patch_energies_kernel(
                             lhsT_scale=v_sc[4:P, i0 : i0 + P],
                             rhs=v2_all[:, S2 * a + j0 : S2 * a + j0 + width].bitcast(FP8X4),
                             rhs_scale=v_sc[:, S2 * a + j0 : S2 * a + j0 + width],
-                            start=(a == 0 and u == 0),
-                            stop=(a == 1 and u == per_bank - 1),
+                            start=(a == order[0] and u == 0),
+                            stop=(a == order[1] and u == per_bank - 1),
                         )
 
         squared = []
@@ -310,7 +310,8 @@ def tile_list_expert_patch_energies_kernel(
         def store_words(j0, j1):
             nc.sync.dma_start(y_words[:, j0:j1], y_w[:, j0:j1].bitcast(I32))
 
-        responses(4)
+        responses(3)
+        responses(1, (1, 0))
         round_w(0)
         round_w(1)
         made = energies(0)

@@ -27,7 +27,7 @@ WIDE = 256
 LAP = 32
 GOT2 = 2 * 4 * PACK * N - LAP
 W4_RAW = GOT2 + S2 - LAP
-PATCH0 = W4_RAW + 4 * N
+FILT1 = W4_RAW + 4 * N
 
 
 def tile_list_expert_patch_energies_kernel(
@@ -53,13 +53,10 @@ def tile_list_expert_patch_energies_kernel(
         nc.sync.dma_start(
             w4_sc_raw[LOW : LOW + ROWS, :].bitcast(I32), w4_scales.rearrange("a q n -> q a n").bitcast(I32)
         )
-        filt = keep.tile([P, 2 * T], I32, name="filt")
-        nc.sync.dma_start(
-            filt[:].rearrange("p (a n) -> p a n", a=2),
-            tab_words.rearrange("a p n i -> p a (n i)").bitcast(I32),
-        )
-        patch = [late.tile([P, T2], I32, name="patch0", offset=PATCH0), keep.tile([P, T2], I32, name="patch1")]
+        filt = [keep.tile([P, T], I32, name="filt0"), late.tile([P, T], I32, name="filt1", offset=FILT1)]
+        patch = [keep.tile([P, T2], I32, name="patch%d" % a) for a in range(2)]
         for a in range(2):
+            nc.sync.dma_start(filt[a][:], tab_words[a].rearrange("p n i -> p (n i)").bitcast(I32))
             nc.sync.dma_start(patch[a][:], tab2_words[a].rearrange("p n i -> p (n i)").bitcast(I32))
         gains = keep.tile([P, 2, 2 * PACK], F32, name="gains")
         nc.sync.dma_start(gains[:, :, 0:PACK], alpha.rearrange("(g p t) -> p g t", g=2, t=PACK))
@@ -99,14 +96,13 @@ def tile_list_expert_patch_energies_kernel(
 
         v_all = keep.tile([P, 2 * S], U32, name="v_all", align_bytes=64)
         v2_all = keep.tile([P, 2 * S2], U32, name="v2_all", align_bytes=64)
-        for g in range(2):
-            for a in range(2):
+        for a in range(2):
+            for g in range(2):
                 nc.vector.tensor_copy(
                     v_all[:, S * a + PASS * g : S * a + PASS * (g + 1)].rearrange("p (t m) -> p m t", t=PACK),
-                    filt[:, a * T : (a + 1) * T].bitcast(U32).indirect(list1[:, 32 * g : 32 * (g + 1)]),
+                    filt[a][:].bitcast(U32).indirect(list1[:, 32 * g : 32 * (g + 1)]),
                 )
-        for a, cuts in enumerate(((0, 512, 1024), (0, 256, 512, 1024))):
-            for j0, j1 in zip(cuts, cuts[1:]):
+            for j0, j1 in ((0, WIDE), (WIDE, S2)):
                 nc.vector.tensor_copy(
                     v2_all[:, S2 * a + j0 : S2 * a + j1],
                     patch[a][:].bitcast(U32).indirect(list2[:, j0 // 16 : j1 // 16]),
@@ -126,7 +122,7 @@ def tile_list_expert_patch_energies_kernel(
                     w4_words.rearrange("a p n -> p a n").bitcast(I32),
                 )
             nc.sync.dma_start(w_raw[-1], w_rows[g, :, :, n0:n1])
-        w4_sc_dealt = late.tile([P, N], U8, name="w4_sc_dealt", offset=PATCH0)
+        w4_sc_dealt = late.tile([P, N], U8, name="w4_sc_dealt", offset=FILT1)
         nc.vector.tensor_copy(
             w4_sc_dealt[:].rearrange("p (t m) -> p m t", t=PACK),
             w4_sc_raw[:].rearrange("p (m t) -> p m t", t=PACK),
@@ -164,11 +160,11 @@ def tile_list_expert_patch_energies_kernel(
             blocks.extend((n, g, j0, width, t0) for g in groups for t0 in range(0, PACK, per_bank))
         banks = []
 
-        def responses(count, order=(0, 1)):
+        def responses(count):
             first = len(banks)
             new = blocks[first : first + count]
             banks.extend(psum.tile([P, BANK], F32, name="bank", tag="a_bank") for block in new)
-            for a in order:
+            for a in range(2):
                 for (n, g, j0, width, t0), bank in zip(new, banks[first:]):
                     per_bank = BANK // width
                     for u in range(per_bank):
@@ -179,8 +175,8 @@ def tile_list_expert_patch_energies_kernel(
                             lhsT_scale=v_sc[4:P, i0 : i0 + P],
                             rhs=v2_all[:, S2 * a + j0 : S2 * a + j0 + width].bitcast(FP8X4),
                             rhs_scale=v_sc[:, S2 * a + j0 : S2 * a + j0 + width],
-                            start=(a == order[0] and u == 0),
-                            stop=(a == order[1] and u == per_bank - 1),
+                            start=(a == 0 and u == 0),
+                            stop=(a == 1 and u == per_bank - 1),
                         )
 
         squared = []
@@ -310,8 +306,7 @@ def tile_list_expert_patch_energies_kernel(
         def store_words(j0, j1):
             nc.sync.dma_start(y_words[:, j0:j1], y_w[:, j0:j1].bitcast(I32))
 
-        responses(3)
-        responses(1, (1, 0))
+        responses(4)
         round_w(0)
         round_w(1)
         made = energies(0)

@@ -85,7 +85,7 @@ def tile_list_expert_patch_energies_kernel(
                     picked[first + 8 * q : first + 8 * (q + 1), :].bitcast(I32),
                 )
 
-        got1 = keep.tile([P, S], U8, name="got1")
+        got1 = keep.tile([P, S], U8, name="got1", align_bytes=64)
         nc.vector.tensor_copy(
             got1[:].rearrange("p (g t m) -> p g m t", g=2, t=PACK), win1[:].indirect(list1[:])
         )
@@ -306,6 +306,12 @@ def tile_list_expert_patch_energies_kernel(
         def store_words(j0, j1):
             nc.sync.dma_start(y_words[:, j0:j1], y_w[:, j0:j1].bitcast(I32))
 
+        warm = [psum.tile([P, BANK], F32, name="warm", tag="a_bank") for n in range(4)]
+        for bank in warm + warm[-1:]:
+            nc.tensor.matmul_mx(
+                bank[:], lhsT=v_all[:, 0:P].bitcast(FP8X4), lhsT_scale=got1[:, 0:P],
+                rhs=v2_all[:, S2 - BANK : S2].bitcast(FP8X4), rhs_scale=got1[:, 0:BANK], start=True, stop=True,
+            )
         responses(4)
         round_w(0)
         round_w(1)

@@ -207,29 +207,36 @@ def tile_list_expert_patch_energies_kernel(
             for c0 in range(0, cols, cut):
                 nc.scalar.activation(ln[:, c0 : c0 + cut], sq[:, c0 : c0 + cut], ACT.Ln, bias=1.0)
             e_bf = ring.tile([P, cols], BF16, name="e_bf", align_bytes=64, bufs=2)
-            half = cols // 2
-            words = half // PACK
-            for u in range(2):
-                if width == WIDE:
-                    src = ln[:].rearrange("p (h j t) -> p j h t", h=2, t=2)[:, words * u : words * (u + 1)]
-                else:
-                    src = ln[:, half * u : half * (u + 1)].rearrange("p (j h t) -> p j h t", h=2, t=2)
-                gain = gains[:, groups[u * len(groups) // 2], 0:PACK].rearrange("p (h t) -> p h t", h=2)
+            if width == WIDE:
                 nc.vector.tensor_tensor(
-                    e_bf[:, half * u : half * (u + 1)].rearrange("p (j h t) -> p j h t", h=2, t=2),
-                    src,
-                    gain.unsqueeze(1).to_broadcast([P, words, 2, 2]),
+                    e_bf[:].rearrange("p (j h t) -> p j h t", h=2, t=2),
+                    ln[:].rearrange("p (h j t) -> p j h t", h=2, t=2),
+                    gains[:, groups[0], 0:PACK].rearrange("p (h t) -> p h t", h=2).unsqueeze(1).to_broadcast([P, WIDE, 2, 2]),
                     MULT,
                 )
+                return e_bf
+            for c0 in range(0, cols, cut):
+                nc.vector.tensor_tensor(
+                    e_bf[:, c0 : c0 + cut].rearrange("p (g j t) -> p g j t", g=len(groups), t=PACK),
+                    ln[:, c0 : c0 + cut].rearrange("p (g j t) -> p g j t", g=len(groups), t=PACK),
+                    gains[:, groups[0] : groups[-1] + 1, 0:PACK].unsqueeze(2).to_broadcast(
+                        [P, len(groups), cut // PACK // len(groups), PACK]
+                    ),
+                    MULT,
+                )
+            return e_bf
+
+        def quantise_e(n, e_bf):
+            j0, width, groups = units[n]
+            cols = PACK * width * len(groups)
+            cut = cols // 2 if n == len(units) - 1 else cols
             e_w = ring.tile([P, cols // PACK], U32, name="e_w", align_bytes=64, bufs=7)
             e_sc = ring.tile([P, cols // PACK], U8, name="e_sc", align_bytes=64, bufs=7)
-            for u in range(2):
-                nc.vector.quantize_mx(
-                    e_w[:, words * u : words * (u + 1)].bitcast(FP8X4), e_sc[:, words * u : words * (u + 1)],
-                    e_bf[:, half * u : half * (u + 1)],
-                )
+            for c0 in range(0, cols, cut):
+                words = slice(c0 // PACK, (c0 + cut) // PACK)
+                nc.vector.quantize_mx(e_w[:, words].bitcast(FP8X4), e_sc[:, words], e_bf[:, c0 : c0 + cut])
             return [
-                (j0, width, g, e_w[:, width * u : width * (u + 1)], e_sc[:, width * u : width * (u + 1)])
+                (g, e_w[:, width * u : width * (u + 1)], e_sc[:, width * u : width * (u + 1)])
                 for u, g in enumerate(groups)
             ]
 
@@ -238,69 +245,75 @@ def tile_list_expert_patch_energies_kernel(
         y_rows = out_0.rearrange("(p t) j -> p t j", t=PACK)
         y_words = out_1[0].rearrange("p m t -> p (m t)").bitcast(I32)
 
-        def mix(j0, width, made, on_vector, per_bank):
+        def mix(j0, width, made, on_scalar, per_bank):
             y = ring.tile([P, PACK, width], F32, name="y", align_bytes=64)
-            for t0 in range(0, PACK, per_bank):
-                bank = psum.tile([P, BANK], F32, name="y_bank", tag="y_bank" if width > P else "a_bank")
-                passes = []
+            firsts = range(0, PACK, per_bank)
+            sums = [psum.tile([P, BANK], F32, name="y_bank", tag="y_bank" if width > P else "a_bank") for t0 in firsts]
+            for t0, bank in zip(firsts, sums):
                 for t in range(t0, t0 + per_bank):
                     for a in range(2):
                         n0 = N * a + P * t
-                        passes.append((
+                        nc.tensor.matmul_mx(
                             bank[:, width * (t - t0) : width * (t - t0 + 1)],
-                            w4_w[:, n0 : n0 + P].bitcast(U8).bitcast(FP4X4),
-                            w4_sc[:, n0 : n0 + P],
-                            v2_all[:, S2 * a + j0 : S2 * a + j0 + width].bitcast(FP8X4),
-                            v_sc[:, S2 * a + j0 : S2 * a + j0 + width],
-                        ))
-                for je, we, g, e_w, e_sc in made:
+                            lhsT=w4_w[:, n0 : n0 + P].bitcast(U8).bitcast(FP4X4),
+                            lhsT_scale=w4_sc[:, n0 : n0 + P],
+                            rhs=v2_all[:, S2 * a + j0 : S2 * a + j0 + width].bitcast(FP8X4),
+                            rhs_scale=v_sc[:, S2 * a + j0 : S2 * a + j0 + width],
+                            start=(t == t0 and a == 0),
+                            stop=False,
+                        )
+            for g, e_w, e_sc in made:
+                for t0, bank in zip(firsts, sums):
                     for t in range(t0, t0 + per_bank):
                         n0 = N * g + P * t
-                        col = width * (t - t0) + je - j0
-                        passes.append((
-                            bank[:, col : col + we],
-                            w_w[:, n0 : n0 + P].bitcast(FP8X4),
-                            w_sc[:, n0 : n0 + P],
-                            e_w.bitcast(FP8X4),
-                            e_sc,
-                        ))
-                for n, (dst, lhs, lhs_sc, rhs, rhs_sc) in enumerate(passes):
-                    nc.tensor.matmul_mx(
-                        dst, lhsT=lhs, lhsT_scale=lhs_sc, rhs=rhs, rhs_scale=rhs_sc,
-                        start=(n == 0), stop=(n == len(passes) - 1),
-                    )
-                if t0 in on_vector:
-                    nc.vector.tensor_tensor(
-                        y[:, t0 : t0 + per_bank, :],
-                        bank[:, 0 : per_bank * width].rearrange("p (t j) -> p t j", j=width),
-                        bias[:, t0 : t0 + per_bank].unsqueeze(2).to_broadcast([P, per_bank, width]),
-                        ADD,
-                    )
-                    continue
-                for t in range(t0, t0 + per_bank):
+                        nc.tensor.matmul_mx(
+                            bank[:, width * (t - t0) : width * (t - t0 + 1)],
+                            lhsT=w_w[:, n0 : n0 + P].bitcast(FP8X4),
+                            lhsT_scale=w_sc[:, n0 : n0 + P],
+                            rhs=e_w.bitcast(FP8X4),
+                            rhs_scale=e_sc,
+                            start=False,
+                            stop=(g == 1 and t == t0 + per_bank - 1),
+                        )
+            for t0, bank in zip(firsts, sums):
+                t1 = t0 + per_bank
+                split = min(max(on_scalar, t0), t1)
+                for t in range(t0, split):
                     nc.scalar.activation(
                         y[:, t, :], bank[:, width * (t - t0) : width * (t - t0 + 1)], ACT.Identity,
                         bias=bias[:, t : t + 1],
                     )
+                if split < t1:
+                    nc.vector.tensor_tensor(
+                        y[:, split:t1, :],
+                        bank[:, width * (split - t0) : width * per_bank].rearrange("p (t j) -> p t j", j=width),
+                        bias[:, split:t1].unsqueeze(2).to_broadcast([P, t1 - split, width]),
+                        ADD,
+                    )
             nc.sync.dma_start(y_rows[:, :, j0 : j0 + width], y[:])
             return y
 
-        def planes(j0, width, y, on_scalar):
-            y_bf = ring.tile([P, PACK * width], BF16, name="y_bf", align_bytes=64)
-            half = width // 2
-            if on_scalar:
-                nc.scalar.copy(y_bf[:].rearrange("p (j t) -> p j t", t=PACK), y[:].rearrange("p t j -> p j t"))
-                nc.vector.quantize_mx(y_w[:, j0 : j0 + width].bitcast(FP8X4), y_sc[:, j0 : j0 + width], y_bf[:])
-                return
-            for c0 in (0, half):
-                nc.vector.tensor_copy(
-                    y_bf[:, PACK * c0 : PACK * (c0 + half)].rearrange("p (c i t) -> p c t i", t=PACK, i=4),
-                    y[:, :, c0 : c0 + half].rearrange("p t (c i) -> p c t i", i=4),
-                )
-            for c0 in (0, half):
+        def round_y(y_bf, y, c0, c1):
+            nc.vector.tensor_copy(
+                y_bf[:, PACK * c0 : PACK * c1].rearrange("p (c i t) -> p c t i", t=PACK, i=4),
+                y[:, :, c0:c1].rearrange("p t (c i) -> p c t i", i=4),
+            )
+
+        def round_y_on_scalar(y_bf, y, c0, c1):
+            nc.scalar.copy(
+                y_bf[:, PACK * c0 : PACK * c1].rearrange("p (c i t) -> p c t i", t=PACK, i=4),
+                y[:, :, c0:c1].rearrange("p t (c i) -> p c t i", i=4),
+            )
+
+        def rounded(width):
+            return ring.tile([P, PACK * width], BF16, name="y_bf", align_bytes=64)
+
+        def quantise_y(j0, width, y_bf, parts):
+            part = width // parts
+            for c0 in range(0, width, part):
                 nc.vector.quantize_mx(
-                    y_w[:, j0 + c0 : j0 + c0 + half].bitcast(FP8X4), y_sc[:, j0 + c0 : j0 + c0 + half],
-                    y_bf[:, PACK * c0 : PACK * (c0 + half)],
+                    y_w[:, j0 + c0 : j0 + c0 + part].bitcast(FP8X4), y_sc[:, j0 + c0 : j0 + c0 + part],
+                    y_bf[:, PACK * c0 : PACK * (c0 + part)],
                 )
 
         def store_words(j0, j1):
@@ -315,25 +328,51 @@ def tile_list_expert_patch_energies_kernel(
         responses(4)
         round_w(0)
         round_w(1)
-        made = energies(0)
+        e_bf = energies(0)
         quantise_w(0)
+        first = quantise_e(0, e_bf)
         deal_w4()
-        made = made + energies(1)
+        e_bf = energies(1)
         round_w(2)
+        first = first + quantise_e(1, e_bf)
+        e_bf = energies(2)
         quantise_w(1)
-        second = energies(2) + energies(3)
-        planes(0, 256, mix(0, 256, made, (2,), 2), False)
-        third = energies(4)
-        planes(256, 256, mix(256, 256, second, (2,), 2), False)
+        second = quantise_e(2, e_bf)
+        e_bf = energies(3)
+        y = mix(0, 256, first, 0, 2)
+        second = second + quantise_e(3, e_bf)
+        y_bf = rounded(256)
+        round_y(y_bf, y, 0, 256)
+        e_bf = energies(4)
+        quantise_y(0, 256, y_bf, 1)
+        third = quantise_e(4, e_bf)
+        y = mix(256, 256, second, 4, 2)
+        e_bf = energies(5)
+        y_bf = rounded(256)
+        round_y(y_bf, y, 0, 256)
+        third = third + quantise_e(5, e_bf)
+        e_bf = energies(6)
+        quantise_y(256, 256, y_bf, 1)
         store_words(0, 512)
-        third = third + energies(5)
-        made = energies(6)
-        y2 = mix(512, 256, third, (), 2)
-        last = energies(7) + energies(8)
-        planes(512, 256, y2, False)
+        fourth = quantise_e(6, e_bf)
+        y = mix(512, 256, third, 4, 2)
+        e_bf = energies(7)
+        e_last = energies(8)
+        last = quantise_e(7, e_bf) + quantise_e(8, e_last)
+        y_bf = rounded(256)
+        round_y(y_bf, y, 0, 128)
+        round_y(y_bf, y, 128, 256)
+        quantise_y(512, 256, y_bf, 2)
         store_words(512, 768)
-        planes(768, 128, mix(768, 128, made, (), 4), True)
-        planes(896, 128, mix(896, 128, last, (2,), 2), False)
+        y = mix(768, 128, fourth, 4, 4)
+        y_bf = rounded(128)
+        round_y_on_scalar(y_bf, y, 0, 128)
+        quantise_y(768, 128, y_bf, 1)
+        y = mix(896, 128, last, 2, 2)
+        y_bf = rounded(128)
+        round_y(y_bf, y, 0, 64)
+        round_y(y_bf, y, 64, 128)
+        quantise_y(896, 128, y_bf, 2)
         store_words(768, S2)
         for q in range(4):
             queue = nc.scalar if q % 2 else nc.sync

from contextlib import ExitStack

import concourse.mybir as mybir

K, T, S, T2, S2, N = 1024, 2048, 1024, 4096, 1024, 512
FLOPS = 2 * K * S * S2 + 2 * S * N * S2 + 2 * K * N * S2

F32 = mybir.dt.float32
BF16 = mybir.dt.bfloat16
I32 = mybir.dt.int32
U32 = mybir.dt.uint32
U16 = mybir.dt.uint16
U8 = mybir.dt.uint8
FP8X4 = mybir.dt.float8_e4m3fn_x4
FP4X4 = mybir.dt.float4_e2m1fn_x4
ACT = mybir.ActivationFunctionType
MULT = mybir.AluOpType.mult
ADD = mybir.AluOpType.add

P = 128
PACK = 4
PASS = 512
BANK = 512
ROWS = 32
LOW, HIGH = 0, 96
WIDE = 256
LAP = 32
GOT2 = 2 * 4 * PACK * N - LAP
W4_RAW = GOT2 + S2 - LAP
FILT1 = W4_RAW + 4 * N


def tile_list_expert_patch_energies_kernel(
    tc, tab_words, tab_scales, tab2_words, tab2_scales, offs, offs2, alpha, w, w4_words, w4_scales, b,
    out_0, out_1, out_2,
):
    nc = tc.nc
    with ExitStack() as ctx:
        keep = ctx.enter_context(tc.tile_pool(name="keep", bufs=1))
        late = ctx.enter_context(tc.tile_pool(name="late", bufs=1))
        ring = ctx.enter_context(tc.tile_pool(name="ring", bufs=3))
        psum = ctx.enter_context(tc.psum_pool(name="psum", bufs=4))

        list1 = keep.tile([P, S // 16], U16, name="list1")
        list2 = keep.tile([P, S2 // 16], U16, name="list2")
        win1 = keep.tile([P, T], U8, name="win1")
        win2 = keep.tile([P, T2], U8, name="win2")
        nc.sync.dma_start(list1[:], offs)
        nc.sync.dma_start(win1[LOW : LOW + ROWS, :].bitcast(I32), tab_scales.rearrange("a q n -> q a n").bitcast(I32))
        nc.sync.dma_start(list2[:], offs2)
        nc.sync.dma_start(win2[HIGH : HIGH + ROWS, :].bitcast(I32), tab2_scales.rearrange("a q n -> q a n").bitcast(I32))
        w4_sc_raw = keep.tile([P, N], U8, name="w4_sc_raw")
        nc.sync.dma_start(
            w4_sc_raw[LOW : LOW + ROWS, :].bitcast(I32), w4_scales.rearrange("a q n -> q a n").bitcast(I32)
        )
        filt = [keep.tile([P, T], I32, name="filt0"), late.tile([P, T], I32, name="filt1", offset=FILT1)]
        patch = [keep.tile([P, T2], I32, name="patch%d" % a) for a in range(2)]
        for a in range(2):
            nc.sync.dma_start(filt[a][:], tab_words[a].rearrange("p n i -> p (n i)").bitcast(I32))
            nc.sync.dma_start(patch[a][:], tab2_words[a].rearrange("p n i -> p (n i)").bitcast(I32))
        gains = keep.tile([P, 2, 2 * PACK], F32, name="gains")
        nc.sync.dma_start(gains[:, :, 0:PACK], alpha.rearrange("(g p t) -> p g t", g=2, t=PACK))

        ones = keep.tile([P, 1], F32, name="ones")
        nc.vector.memset(ones[:], 1.0)
        for p0, p1 in ((32, 64), (64, P)):
            nc.vector.memset(win1[p0:p1, :].bitcast(I32), 0)
        nc.vector.memset(win2[0:HIGH, :].bitcast(I32), 0)
        v_sc = keep.tile([P, 2 * S2], U8, name="v_sc", align_bytes=64)
        nc.vector.memset(v_sc[:].bitcast(I32), 0)
        zero = keep.tile([P, 1], F32, name="zero")
        nc.scalar.activation(zero[:], ones[:], ACT.Ln)

        w4_sc = keep.tile([P, 2 * N], U8, name="w4_sc", align_bytes=64)
        for p0, p1 in ((32, 64), (64, P)):
            nc.vector.memset(w4_sc_raw[p0:p1, :].bitcast(I32), 0)
        nc.vector.memset(w4_sc[:].bitcast(I32), 0)
        bias = keep.tile([P, PACK], F32, name="bias")
        nc.gpsimd.dma_start(bias[:], b.rearrange("(p t) -> p t", t=PACK))

        def place(queue, planes, row, picked, first):
            for q in (0, 2, 1, 3):
                queue.dma_start(
                    planes[32 * q + row : 32 * q + row + 4, :].bitcast(I32).rearrange("r (a n) -> r a n", a=2),
                    picked[first + 8 * q : first + 8 * (q + 1), :].bitcast(I32),
                )

        got1 = keep.tile([P, S], U8, name="got1", align_bytes=64)
        nc.vector.tensor_copy(
            got1[:].rearrange("p (g t m) -> p g m t", g=2, t=PACK), win1[:].indirect(list1[:])
        )
        place(nc.gpsimd, v_sc, 4, got1, LOW)
        got2 = late.tile([P, S2], U8, name="got2", offset=GOT2)
        nc.vector.tensor_copy(got2[:], win2[:].indirect(list2[:]))
        place(nc.scalar, v_sc, 0, got2, HIGH)

        v_all = keep.tile([P, 2 * S], U32, name="v_all", align_bytes=64)
        v2_all = keep.tile([P, 2 * S2], U32, name="v2_all", align_bytes=64)
        for a in range(2):
            for g in range(2):
                nc.vector.tensor_copy(
                    v_all[:, S * a + PASS * g : S * a + PASS * (g + 1)].rearrange("p (t m) -> p m t", t=PACK),
                    filt[a][:].bitcast(U32).indirect(list1[:, 32 * g : 32 * (g + 1)]),
                )
            for j0, j1 in ((0, WIDE), (WIDE, S2)):
                nc.vector.tensor_copy(
                    v2_all[:, S2 * a + j0 : S2 * a + j1],
                    patch[a][:].bitcast(U32).indirect(list2[:, j0 // 16 : j1 // 16]),
                )

        w_all = late.tile([P, 2 * PACK * N], F32, name="w_all", offset=0)
        w_rows = w.rearrange("(g p s) n -> g p s n", g=2, s=PACK)
        w_parts = ((0, 0, N // 2), (0, N // 2, N), (1, 0, N))
        w_raw = []
        for g, n0, n1 in w_parts:
            c0 = PACK * (N * g + n0)
            w_raw.append(w_all[:, c0 : c0 + PACK * (n1 - n0)].rearrange("p (s n) -> p s n", s=PACK))
            if g == 1:
                w4_raw = late.tile([P, 2 * N], U16, name="w4_raw", offset=W4_RAW)
                nc.sync.dma_start(
                    w4_raw[:].bitcast(I32).rearrange("p (a n) -> p a n", a=2),
                    w4_words.rearrange("a p n -> p a n").bitcast(I32),
                )
            nc.sync.dma_start(w_raw[-1], w_rows[g, :, :, n0:n1])
        w4_sc_dealt = late.tile([P, N], U8, name="w4_sc_dealt", offset=FILT1)
        nc.vector.tensor_copy(
            w4_sc_dealt[:].rearrange("p (t m) -> p m t", t=PACK),
            w4_sc_raw[:].rearrange("p (m t) -> p m t", t=PACK),
        )
        place(nc.sync, w4_sc, 0, w4_sc_dealt, LOW)

        w4_w = keep.tile([P, 2 * N], U16, name="w4_w", align_bytes=64)
        w_w = keep.tile([P, 2 * N], U32, name="w_w", align_bytes=64)
        w_sc = keep.tile([P, 2 * N], U8, name="w_sc", align_bytes=64)
        w_bf = [keep.tile([P, PACK * N], BF16, name="w_bf%d" % g, align_bytes=64) for g in range(2)]

        def deal_w4():
            nc.vector.tensor_copy(
                w4_w[:].rearrange("p (a t m) -> p a m t", a=2, t=PACK),
                w4_raw[:].rearrange("p (a m t) -> p a m t", a=2, t=PACK),
            )

        def round_w(part):
            g, n0, n1 = w_parts[part]
            nc.vector.tensor_copy(
                w_bf[g][:].rearrange("p (t m s) -> p m s t", t=PACK, s=PACK)[:, n0 // PACK : n1 // PACK],
                w_raw[part].rearrange("p s (m t) -> p m s t", t=PACK),
            )

        def quantise_w(g):
            nc.vector.quantize_mx(
                w_w[:, N * g : N * (g + 1)].bitcast(FP8X4), w_sc[:, N * g : N * (g + 1)], w_bf[g][:]
            )

        units = [(j0, WIDE, (g,)) for j0 in (0, 256, 512) for g in range(2)]
        units = units + [(768, P, (0, 1)), (896, P, (0,)), (896, P, (1,))]
        blocks = []
        for n, (j0, width, groups) in enumerate(units):
            per_bank = BANK // width
            blocks.extend((n, g, j0, width, t0) for g in groups for t0 in range(0, PACK, per_bank))
        banks = []

        def responses(count):
            first = len(banks)
            new = blocks[first : first + count]
            banks.extend(psum.tile([P, BANK], F32, name="bank", tag="a_bank") for block in new)
            for a in range(2):
                for (n, g, j0, width, t0), bank in zip(new, banks[first:]):
                    per_bank = BANK // width
                    for u in range(per_bank):
                        i0 = S * a + PASS * g + P * (t0 + u)
                        nc.tensor.matmul_mx(
                            bank[:, width * u : width * (u + 1)],
                            lhsT=v_all[:, i0 : i0 + P].bitcast(FP8X4),
                            lhsT_scale=v_sc[4:P, i0 : i0 + P],
                            rhs=v2_all[:, S2 * a + j0 : S2 * a + j0 + width].bitcast(FP8X4),
                            rhs_scale=v_sc[:, S2 * a + j0 : S2 * a + j0 + width],
                            start=(a == 0 and u == 0),
                            stop=(a == 1 and u == per_bank - 1),
                        )

        squared = []
        sq_tiles = {}

        def square():
            n, g, j0, width, t0 = blocks[len(squared)]
            u = squared.count(n)
            if u == 0:
                sq_tiles[n] = ring.tile([P, PACK * width * len(units[n][2])], F32, name="sq", align_bytes=64, bufs=2)
            nc.scalar.activation(
                sq_tiles[n][:, BANK * u : BANK * (u + 1)].rearrange("p (j t) -> p j t", j=width),
                banks[len(squared)][:].rearrange("p (t j) -> p j t", j=width),
                ACT.Square,
                bias=0.0 if squared else zero[:],
            )
            squared.append(n)
            responses(1)

        def energies(n):
            j0, width, groups = units[n]
            cols = PACK * width * len(groups)
            while len(squared) < len(blocks) and n + 1 not in squared:
                square()
            sq = sq_tiles[n]
            ln = ring.tile([P, cols], F32, name="ln", align_bytes=64, bufs=4)
            cut = cols // 2 if n == len(units) - 1 else cols
            for c0 in range(0, cols, cut):
                nc.scalar.activation(ln[:, c0 : c0 + cut], sq[:, c0 : c0 + cut], ACT.Ln, bias=1.0)
            e_bf = ring.tile([P, cols], BF16, name="e_bf", align_bytes=64, bufs=2)
            if width == WIDE:
                nc.vector.tensor_tensor(
                    e_bf[:].rearrange("p (j h t) -> p j h t", h=2, t=2),
                    ln[:].rearrange("p (h j t) -> p j h t", h=2, t=2),
                    gains[:, groups[0], 0:PACK].rearrange("p (h t) -> p h t", h=2).unsqueeze(1).to_broadcast([P, WIDE, 2, 2]),
                    MULT,
                )
                return e_bf
            for c0 in range(0, cols, cut):
                nc.vector.tensor_tensor(
                    e_bf[:, c0 : c0 + cut].rearrange("p (g j t) -> p g j t", g=len(groups), t=PACK),
                    ln[:, c0 : c0 + cut].rearrange("p (g j t) -> p g j t", g=len(groups), t=PACK),
                    gains[:, groups[0] : groups[-1] + 1, 0:PACK].unsqueeze(2).to_broadcast(
                        [P, len(groups), cut // PACK // len(groups), PACK]
                    ),
                    MULT,
                )
            return e_bf

        def quantise_e(n, e_bf):
            j0, width, groups = units[n]
            cols = PACK * width * len(groups)
            cut = cols // 2 if n == len(units) - 1 else cols
            e_w = ring.tile([P, cols // PACK], U32, name="e_w", align_bytes=64, bufs=7)
            e_sc = ring.tile([P, cols // PACK], U8, name="e_sc", align_bytes=64, bufs=7)
            for c0 in range(0, cols, cut):
                words = slice(c0 // PACK, (c0 + cut) // PACK)
                nc.vector.quantize_mx(e_w[:, words].bitcast(FP8X4), e_sc[:, words], e_bf[:, c0 : c0 + cut])
            return [
                (g, e_w[:, width * u : width * (u + 1)], e_sc[:, width * u : width * (u + 1)])
                for u, g in enumerate(groups)
            ]

        y_w = keep.tile([P, S2], U32, name="y_w", align_bytes=64)
        y_sc = keep.tile([P, S2], U8, name="y_sc", align_bytes=64)
        y_rows = out_0.rearrange("(p t) j -> p t j", t=PACK)
        y_words = out_1[0].rearrange("p m t -> p (m t)").bitcast(I32)

        def mix(j0, width, made, on_scalar, per_bank):
            y = ring.tile([P, PACK, width], F32, name="y", align_bytes=64)
            firsts = range(0, PACK, per_bank)
            sums = [psum.tile([P, BANK], F32, name="y_bank", tag="y_bank" if width > P else "a_bank") for t0 in firsts]
            for t0, bank in zip(firsts, sums):
                for t in range(t0, t0 + per_bank):
                    for a in range(2):
                        n0 = N * a + P * t
                        nc.tensor.matmul_mx(
                            bank[:, width * (t - t0) : width * (t - t0 + 1)],
                            lhsT=w4_w[:, n0 : n0 + P].bitcast(U8).bitcast(FP4X4),
                            lhsT_scale=w4_sc[:, n0 : n0 + P],
                            rhs=v2_all[:, S2 * a + j0 : S2 * a + j0 + width].bitcast(FP8X4),
                            rhs_scale=v_sc[:, S2 * a + j0 : S2 * a + j0 + width],
                            start=(t == t0 and a == 0),
                            stop=False,
                        )
            for g, e_w, e_sc in made:
                for t0, bank in zip(firsts, sums):
                    for t in range(t0, t0 + per_bank):
                        n0 = N * g + P * t
                        nc.tensor.matmul_mx(
                            bank[:, width * (t - t0) : width * (t - t0 + 1)],
                            lhsT=w_w[:, n0 : n0 + P].bitcast(FP8X4),
                            lhsT_scale=w_sc[:, n0 : n0 + P],
                            rhs=e_w.bitcast(FP8X4),
                            rhs_scale=e_sc,
                            start=False,
                            stop=(g == 1 and t == t0 + per_bank - 1),
                        )
            for t0, bank in zip(firsts, sums):
                t1 = t0 + per_bank
                split = min(max(on_scalar, t0), t1)
                for t in range(t0, split):
                    nc.scalar.activation(
                        y[:, t, :], bank[:, width * (t - t0) : width * (t - t0 + 1)], ACT.Identity,
                        bias=bias[:, t : t + 1],
                    )
                if split < t1:
                    nc.vector.tensor_tensor(
                        y[:, split:t1, :],
                        bank[:, width * (split - t0) : width * per_bank].rearrange("p (t j) -> p t j", j=width),
                        bias[:, split:t1].unsqueeze(2).to_broadcast([P, t1 - split, width]),
                        ADD,
                    )
            nc.sync.dma_start(y_rows[:, :, j0 : j0 + width], y[:])
            return y

        def round_y(y_bf, y, c0, c1):
            nc.vector.tensor_copy(
                y_bf[:, PACK * c0 : PACK * c1].rearrange("p (c i t) -> p c t i", t=PACK, i=4),
                y[:, :, c0:c1].rearrange("p t (c i) -> p c t i", i=4),
            )

        def round_y_on_scalar(y_bf, y, c0, c1):
            nc.scalar.copy(
                y_bf[:, PACK * c0 : PACK * c1].rearrange("p (c i t) -> p c t i", t=PACK, i=4),
                y[:, :, c0:c1].rearrange("p t (c i) -> p c t i", i=4),
            )

        def rounded(width):
            return ring.tile([P, PACK * width], BF16, name="y_bf", align_bytes=64)

        def quantise_y(j0, width, y_bf, parts):
            part = width // parts
            for c0 in range(0, width, part):
                nc.vector.quantize_mx(
                    y_w[:, j0 + c0 : j0 + c0 + part].bitcast(FP8X4), y_sc[:, j0 + c0 : j0 + c0 + part],
                    y_bf[:, PACK * c0 : PACK * (c0 + part)],
                )

        def store_words(j0, j1):
            nc.sync.dma_start(y_words[:, j0:j1], y_w[:, j0:j1].bitcast(I32))

        warm = [psum.tile([P, BANK], F32, name="warm", tag="a_bank") for n in range(4)]
        for bank in warm + warm[-1:]:
            nc.tensor.matmul_mx(
                bank[:], lhsT=v_all[:, 0:P].bitcast(FP8X4), lhsT_scale=got1[:, 0:P],
                rhs=v2_all[:, S2 - BANK : S2].bitcast(FP8X4), rhs_scale=got1[:, 0:BANK], start=True, stop=True,
            )
        responses(4)
        round_w(0)
        round_w(1)
        e_bf = energies(0)
        quantise_w(0)
        first = quantise_e(0, e_bf)
        deal_w4()
        e_bf = energies(1)
        round_w(2)
        first = first + quantise_e(1, e_bf)
        e_bf = energies(2)
        quantise_w(1)
        second = quantise_e(2, e_bf)
        e_bf = energies(3)
        y = mix(0, 256, first, 0, 2)
        second = second + quantise_e(3, e_bf)
        y_bf = rounded(256)
        round_y(y_bf, y, 0, 256)
        e_bf = energies(4)
        quantise_y(0, 256, y_bf, 1)
        third = quantise_e(4, e_bf)
        y = mix(256, 256, second, 4, 2)
        e_bf = energies(5)
        y_bf = rounded(256)
        round_y(y_bf, y, 0, 256)
        third = third + quantise_e(5, e_bf)
        e_bf = energies(6)
        quantise_y(256, 256, y_bf, 1)
        store_words(0, 512)
        fourth = quantise_e(6, e_bf)
        y = mix(512, 256, third, 4, 2)
        e_bf = energies(7)
        e_last = energies(8)
        last = quantise_e(7, e_bf) + quantise_e(8, e_last)
        y_bf = rounded(256)
        round_y(y_bf, y, 0, 128)
        round_y(y_bf, y, 128, 256)
        quantise_y(512, 256, y_bf, 2)
        store_words(512, 768)
        y = mix(768, 128, fourth, 4, 4)
        y_bf = rounded(128)
        round_y_on_scalar(y_bf, y, 0, 128)
        quantise_y(768, 128, y_bf, 1)
        y = mix(896, 128, last, 2, 2)
        y_bf = rounded(128)
        round_y(y_bf, y, 0, 64)
        round_y(y_bf, y, 64, 128)
        quantise_y(896, 128, y_bf, 2)
        store_words(768, S2)
        for q in range(4):
            queue = nc.scalar if q % 2 else nc.sync
            queue.dma_start(
                out_2[0, 4 * q : 4 * q + 4, :].bitcast(I32), y_sc[32 * q : 32 * q + 4, :].bitcast(I32)
            )
